import numpy as np
import ml_dtypes


def mxq(x, axis, fmt="e4m3"):
    dtype, down = {"e4m3": (ml_dtypes.float8_e4m3fn, 7), "e5m2": (ml_dtypes.float8_e5m2, 14)}[fmt]
    v = np.moveaxis(np.asarray(x, np.float32).astype(ml_dtypes.bfloat16).astype(np.float64), axis, -1)
    blocks = v.reshape(v.shape[:-1] + (-1, 32))
    amax = np.abs(blocks).max(-1, keepdims=True)
    byte = np.maximum(np.where(amax > 0, np.frexp(amax)[1] - 1 + 127, 0) - down, 1)
    scale = np.exp2(byte - 127.0)
    codes = (blocks / scale).astype(np.float32).astype(dtype).astype(np.float64)
    return np.moveaxis((codes * scale).reshape(v.shape), -1, axis)


WIDE = False


def mx_kscale(k):
    if not WIDE:
        return np.ones(k)
    levels = np.array([10, -10, 5, -5, 0])
    if k % 512:
        return np.exp2(np.random.permutation(np.resize(levels, k // 32))).repeat(32)
    a = np.empty((k // 512, 16))
    for p in range(k // 512):
        a[p, :8] = np.random.permutation(np.resize(levels, 8))
        for g in range(8):
            far = levels[np.abs(levels - a[p, g]) >= 10]
            a[p, g + 8] = far[np.random.randint(len(far))]
    return np.exp2(a.ravel()).repeat(32)


def f64(x):
    return np.asarray(x).astype(np.float64)


def striped(idx):
    return np.tile(idx.reshape(-1, 16).T, (8, 1)).astype(np.uint16)


def unstriped(offs):
    return offs[:16].T.reshape(-1).astype(np.int64)


E2M1 = np.array([0.0, 0.5, 1.0, 1.5, 2.0, 3.0, 4.0, 6.0, -0.0, -0.5, -1.0, -1.5, -2.0, -3.0, -4.0, -6.0])


def pack_weight(w, fmt):
    k, n = w.shape
    w = f64(np.asarray(w, np.float32).astype(ml_dtypes.bfloat16)).reshape(k // 32, 32, n)
    amax = np.abs(w).max(1)
    if fmt == "e4m3":
        byte = np.frexp(amax)[1] - 1 + 127 - 7
    else:
        mant, ex = np.frexp(amax / 6.0)
        byte = np.where(mant > 0.5, ex, ex - 1) + 127
    byte = np.clip(np.where(amax > 0, byte, 1), 1, 254)
    scaled = (w * np.exp2(127.0 - byte)[:, None, :]).reshape(k, n).astype(np.float32)
    by_word = np.ascontiguousarray(scaled.reshape(k // 512, 128, 4, n).transpose(0, 1, 3, 2))
    if fmt == "e4m3":
        words = by_word.astype(ml_dtypes.float8_e4m3fn).view(np.uint8)
    else:
        c = by_word.astype(ml_dtypes.float4_e2m1fn).view(np.uint8) & 0xF
        words = (c[..., 0::2] | (c[..., 1::2] << 4)).reshape(k // 512, 128, 2 * n)
    return np.ascontiguousarray(words), np.ascontiguousarray(byte.astype(np.uint8).reshape(k // 512, 16, n))


def unpack_weight(words, scales, fmt):
    g, _, n = scales.shape
    words = np.ascontiguousarray(words).reshape(g, 128, n, -1)
    if fmt == "e4m3":
        vals = words.view(ml_dtypes.float8_e4m3fn).astype(np.float64)
    else:
        nib = np.empty((g, 128, n, 4), np.uint8)
        nib[..., 0::2] = words & 0xF
        nib[..., 1::2] = words >> 4
        vals = E2M1[nib]
    vals = vals * np.repeat(np.exp2(scales.astype(np.float64) - 127.0), 8, axis=1)[..., None]
    return vals.transpose(0, 1, 3, 2).reshape(g * 512, n)


def gelu(v):
    return 0.5 * v * (1.0 + np.tanh(np.sqrt(2.0 / np.pi) * (v + 0.044715 * v**3)))


K, T, S, H, T2, P = 1024, 4096, 1024, 512, 2048, 1024

def setup_inputs():
    n = np.random.standard_normal
    s = mx_kscale(K)[:, None]
    u = mx_kscale(H)[:, None]
    d = {}
    d["tab_words"], d["tab_scales"] = pack_weight(n((K, T)) * s, "e4m3")
    d["offs"] = striped(np.random.permutation(T)[:S])
    d["offs2"] = striped(np.random.permutation(T2)[:S])
    d["offs3"] = striped(np.random.permutation(T2)[:P])
    d["offs4"] = striped(np.random.permutation(T2)[:P])
    d["w1_words"], d["w1_scales"] = pack_weight(1.6 * n((K, H)) / K ** 0.5 / s, "e2m1")
    d["w2"] = (0.55 * n((K, H)) / K ** 0.5 / s).astype(np.float32)
    d["w3"] = (0.7 * n((K, H)) / K ** 0.5 / s).astype(np.float32)
    d["gain"] = (0.8 * np.exp(0.3 * n(H)) * u[:, 0]).astype(np.float32)
    d["wgs"] = np.exp(0.3 * n((128, S))).astype(np.float32)
    d["page0"] = (n((H, T2)) * u).astype(np.float32)
    d["aim"] = (0.7 * n((H, P)) * u).astype(np.float32)
    d["w4"] = (0.8 * n((H, H)) / H ** 0.5 / u / u.T).astype(np.float32)
    d["wgo"] = np.exp(0.3 * n((128, P))).astype(np.float32)
    d["page1"] = n((H, T2)).astype(np.float32)
    return d

def reference(tab_words, tab_scales, offs, offs2, offs3, offs4, w1_words, w1_scales, w2, w3, gain, wgs, page0, aim, w4, wgo, page1):
    v = unpack_weight(tab_words, tab_scales, "e4m3")[:, unstriped(offs)]
    w1 = unpack_weight(w1_words, w1_scales, "e2m1")
    a = np.tanh(w1.T @ v)
    b = np.cos(mxq(f64(w2), 0, "e4m3").T @ v)
    e = mxq(f64(w3), 0, "e4m3").T @ v
    h = (a + b + e) * f64(gain)[:, None]
    page = f64(page0).copy()
    page[:, unstriped(offs2)] = np.tile(f64(wgs), (H // 128, 1)) * h
    x = page[:, unstriped(offs3)] - f64(aim)
    y = (mxq(f64(w4), 0, "e4m3").T @ mxq(x, 0, "e4m3")) * x
    out = f64(page1).copy()
    out[:, unstriped(offs4)] = np.tile(f64(wgo), (H // 128, 1)) * y
    return out

@@ -1,0 +1,265 @@
+import math
+from contextlib import ExitStack
+
+import concourse.mybir as mybir
+from concourse.masks import make_identity
+
+K, T, S, H, T2, PN = 1024, 4096, 1024, 512, 2048, 1024
+FLOPS = 2 * (3 * K * H * S + H * H * PN)
+
+F32 = mybir.dt.float32
+BF16 = mybir.dt.bfloat16
+I32 = mybir.dt.int32
+U32 = mybir.dt.uint32
+U16 = mybir.dt.uint16
+U8 = mybir.dt.uint8
+FP8X4 = mybir.dt.float8_e4m3fn_x4
+FP4X4 = mybir.dt.float4_e2m1fn_x4
+ALU = mybir.AluOpType
+ACT = mybir.ActivationFunctionType
+
+P = 128
+PACK = 4
+K_PASS = P * PACK
+PASSES = K // K_PASS
+TILES = H // P
+CHUNK = 256
+STAGE2_CHUNKS = ((0, 256), (256, 512), (512, 1024))
+HALF = H // 2
+
+
+def tile_list_falcon_ration_features_kernel(
+    tc, tab_words, tab_scales, offs, offs2, offs3, offs4, w1_words, w1_scales, w2, w3, gain, wgs, page0, aim, w4, wgo, page1, out
+):
+    nc = tc.nc
+    with ExitStack() as ctx:
+        lists = ctx.enter_context(tc.tile_pool(name="lists", bufs=1))
+        keep = ctx.enter_context(tc.tile_pool(name="keep", bufs=1))
+        work = ctx.enter_context(tc.tile_pool(name="work", bufs=1))
+        psum = ctx.enter_context(tc.psum_pool(name="psum", bufs=1))
+
+        idx1 = lists.tile([P, S // 16], U16, name="idx1")
+        idx2 = lists.tile([P, S // 16], U16, name="idx2")
+        idx3 = lists.tile([P, PN // 16], U16, name="idx3")
+        idx4 = lists.tile([P, PN // 16], U16, name="idx4")
+
+        def entries(idx, lo, hi):
+            return idx[:, lo // 16 : hi // 16]
+
+        tab_sc = keep.tile([P, T], U8, name="tab_sc", align_bytes=64)
+        nc.vector.memset(tab_sc[:].bitcast(I32), 0)
+        zero = keep.tile([P, 1], F32, name="zero")
+        nc.vector.memset(zero[:], 0.0)
+        zero_bias = keep.tile([P, 1], F32, name="zero_bias")
+        nc.scalar.activation(zero_bias[:], zero[:], ACT.Silu)
+
+        w1_sc = keep.tile([P, PASSES, H], U8, name="w1_sc", align_bytes=64)
+        nc.gpsimd.memset(w1_sc[:].rearrange("p a c -> p (a c)").bitcast(I32), 0)
+        v_sc_moved = keep.tile([P, S], U8, name="v_sc_moved", align_bytes=64)
+        nc.gpsimd.memset(v_sc_moved[:].bitcast(I32), 0)
+        ident = keep.tile([P, P], F32, name="ident")
+        make_identity(nc, ident[:])
+
+        nc.sync.dma_start(idx1[:], offs)
+        tab = [keep.tile([P, T], I32, name=f"tab{a}") for a in range(PASSES)]
+        for a in range(PASSES):
+            nc.sync.dma_start(tab[a][:], tab_words[a].rearrange("p t i -> p (t i)").bitcast(I32))
+            if a == 0:
+                for q in range(4):
+                    nc.sync.dma_start(
+                        tab_sc[32 * q : 32 * q + 8, :].bitcast(I32), tab_scales[:, 4 * q : 4 * q + 4, :].bitcast(I32)
+                    )
+
+        def load_weight_pass(w, a):
+            raw = work.tile([P, PACK, H], F32, name="raw", tag="raw", bufs=4)
+            nc.sync.dma_start(raw[:], w[a * K_PASS : (a + 1) * K_PASS, :].rearrange("(p i) c -> p i c", i=PACK))
+            return raw
+
+        w2_raw = [load_weight_pass(w2, a) for a in range(PASSES)]
+        w1_codes = keep.tile([P, PASSES, 2 * H], U8, name="w1_codes", align_bytes=64)
+        nc.sync.dma_start(w1_codes[:].bitcast(I32), w1_words.rearrange("a p c -> p a c").bitcast(I32))
+        picked_sc = keep.tile([P, S], U8, name="picked_sc", align_bytes=64)
+        nc.vector.tensor_copy(picked_sc[:], tab_sc[:].indirect(idx1[:]))
+        for q in range(4):
+            nc.sync.dma_start(
+                v_sc_moved[32 * q : 32 * q + 4, :].bitcast(I32), picked_sc[32 * q + 4 : 32 * q + 8, :].bitcast(I32)
+            )
+        w3_raw = [load_weight_pass(w3, a) for a in range(PASSES)]
+        nc.sync.dma_start(idx2[:], offs2)
+        wgs_sb = keep.tile([P, S], F32, name="wgs_sb")
+        nc.sync.dma_start(wgs_sb[:], wgs)
+        page = [keep.tile([P, T2], F32, name=f"page{t}") for t in range(TILES)]
+        for t in range(TILES):
+            nc.sync.dma_start(page[t][:], page0[t * P : (t + 1) * P, :])
+        nc.sync.dma_start(idx3[:], offs3)
+        nc.sync.dma_start(idx4[:], offs4)
+
+        for q in range(4):
+            nc.gpsimd.dma_start(
+                w1_sc[32 * q : 32 * q + 4, :, :].bitcast(I32),
+                w1_scales[:, 4 * q : 4 * q + 4, :].rearrange("a r c -> r a c").bitcast(I32),
+            )
+        gain_sb = keep.tile([P, TILES], F32, name="gain_sb")
+        with nc.allow_non_contiguous_dma(reason="one gain value for each partition and tile"):
+            nc.gpsimd.dma_start(gain_sb[:], gain.rearrange("(t p) -> p t", p=P))
+        neg_gain = keep.tile([P, TILES], F32, name="neg_gain")
+        nc.gpsimd.tensor_scalar(neg_gain[:], gain_sb[:], -1.0, 0.0, ALU.mult, ALU.add)
+
+        v = [keep.tile([P, S], U32, name=f"v{a}", align_bytes=64) for a in range(PASSES)]
+        for a in range(PASSES):
+            nc.vector.tensor_copy(v[a][:], tab[a][:].bitcast(U32).indirect(idx1[:]))
+
+        def quantise_weight(raw, codes, scales, engines):
+            for half in range(2):
+                cols = slice(half * HALF, (half + 1) * HALF)
+                grouped = work.tile([P, HALF, PACK], BF16, name="grouped", tag="grouped", bufs=4, align_bytes=64)
+                dst = grouped[:].rearrange("p (c e) i -> p c i e", e=4)
+                src = raw[:, :, cols].rearrange("p i (c e) -> p c i e", e=4)
+                if engines[half] == "vector":
+                    nc.vector.tensor_copy(dst, src)
+                else:
+                    nc.scalar.copy(dst, src)
+                nc.vector.quantize_mx(
+                    codes[:, cols].bitcast(FP8X4), scales[:, cols], grouped[:].rearrange("p c i -> p (c i)")
+                )
+
+        def mx_tiles(name, width):
+            codes = keep.tile([P, width], U32, name=name + "_codes", align_bytes=64)
+            scales = keep.tile([P, width], U8, name=name + "_sc", align_bytes=64)
+            return codes, scales
+
+        w2_q = [mx_tiles(f"w2_{a}", H) for a in range(PASSES)]
+        w3_q = [mx_tiles(f"w3_{a}", H) for a in range(PASSES)]
+        for a in range(PASSES):
+            quantise_weight(w2_raw[a], w2_q[a][0], w2_q[a][1], ("vector", "scalar"))
+
+        v_sc_packed = [picked_sc[4 * a : P, :] for a in range(PASSES)]
+        v_sc_plain = [picked_sc[:], v_sc_moved[:]]
+
+        def first_product(jb, moving, v_sc):
+            bank = psum.tile([P, H], F32, name="bank", tag="mm", bufs=5)
+            cols = slice(jb * P, (jb + 1) * P)
+            for a in range(PASSES):
+                codes, scales = moving[a]
+                nc.tensor.matmul_mx(
+                    bank[:], lhsT=v[a][:, cols].bitcast(FP8X4), lhsT_scale=v_sc[a][:, cols],
+                    rhs=codes, rhs_scale=scales, start=(a == 0), stop=(a == PASSES - 1),
+                )
+            return bank
+
+        w1_mv = [(w1_codes[:, a, :].bitcast(FP4X4), w1_sc[:, a, :]) for a in range(PASSES)]
+        w2_mv = [(w2_q[a][0][:].bitcast(FP8X4), w2_q[a][1][:]) for a in range(PASSES)]
+        w3_mv = [(w3_q[a][0][:].bitcast(FP8X4), w3_q[a][1][:]) for a in range(PASSES)]
+
+        def reduced_angle(jb, angle):
+            bank = first_product(jb, w2_mv, v_sc_packed)
+            turns = work.tile([P, H], I32, name="turns", tag="turns", bufs=2)
+            nc.vector.tensor_scalar(turns[:], bank[:], 1.0 / (2.0 * math.pi), None, ALU.mult)
+            nc.vector.scalar_tensor_tensor(angle, turns[:], -2.0 * math.pi, bank[:], ALU.mult, ALU.add)
+
+        per_chunk = CHUNK // P
+
+        def reduced_angles(c):
+            both = work.tile([P, per_chunk, H], F32, name="angles", tag="wide", bufs=4)
+            for b in range(per_chunk):
+                reduced_angle(c * per_chunk + b, both[:, b, :])
+            return both
+
+        angles = [reduced_angles(0)]
+        quantise_weight(w3_raw[0], w3_q[0][0], w3_q[0][1], ("scalar", "scalar"))
+        quantise_weight(w3_raw[1], w3_q[1][0], w3_q[1][1], ("vector", "scalar"))
+
+        aim_sb = []
+        for pair in range(TILES // 2):
+            aim_pair = work.tile([P, 2, PN], F32, name="aim_pair", tag="raw", bufs=4)
+            nc.sync.dma_start(aim_pair[:], aim[2 * pair * P : (2 * pair + 2) * P, :].rearrange("(t p) j -> p t j", p=P))
+            aim_sb.extend([aim_pair[:, 0, :], aim_pair[:, 1, :]])
+        w4_raw = load_weight_pass(w4, 0)
+        wgo_sb = keep.tile([P, PN], F32, name="wgo_sb")
+        nc.sync.dma_start(wgo_sb[:], wgo)
+        ration = [keep.tile([P, T2], F32, name=f"ration{t}") for t in range(TILES)]
+        for t in range(TILES):
+            nc.sync.dma_start(ration[t][:], page1[t * P : (t + 1) * P, :])
+
+        for c in range(S // CHUNK):
+            terms = []
+            for b in range(per_chunk):
+                jb = c * per_chunk + b
+                bank = first_product(jb, w1_mv, v_sc_plain)
+                bounded = work.tile([P, H], F32, name="bounded", tag="bounded", bufs=4)
+                nc.scalar.activation(bounded[:], bank[:], ACT.Tanh, bias=zero_bias[:], scale=-1.0)
+                wave = work.tile([P, H], F32, name="wave", tag="wave", bufs=4)
+                nc.scalar.activation(wave[:], angles[c][:, b, :], ACT.Sin, bias=zero_bias[:], scale=0.5)
+                nc.scalar.activation(wave[:], wave[:], ACT.Square, bias=zero_bias[:], scale=math.sqrt(2.0))
+                bank = first_product(jb, w3_mv, v_sc_packed)
+                bare = work.tile([P, H], F32, name="bare", tag="bare", bufs=4)
+                nc.scalar.activation(bare[:], bank[:], ACT.Copy, bias=-1.0, scale=-1.0)
+                terms.append((bounded, wave, bare))
+            for t in range(TILES):
+                rows = slice(t * P, (t + 1) * P)
+                total = psum.tile([P, CHUNK], F32, name="total", tag="tr", bufs=3)
+                for b in range(per_chunk):
+                    for n, term in enumerate(terms[b]):
+                        nc.tensor.matmul(
+                            total[:, b * P : (b + 1) * P], lhsT=term[:, rows], rhs=ident[:],
+                            is_transpose=True, start=(n == 0), stop=(n == 2),
+                        )
+                h = work.tile([P, CHUNK], F32, name="h", tag="h", bufs=6, align_bytes=64)
+                nc.scalar.activation(h[:], total[:], ACT.Copy, scale=neg_gain[:, t : t + 1])
+                lo, hi = c * CHUNK, (c + 1) * CHUNK
+                nc.vector.tensor_tensor(page[t][:].indirect(entries(idx2, lo, hi)), h[:], wgs_sb[:, lo:hi], ALU.mult)
+            if c + 1 < S // CHUNK:
+                angles.append(reduced_angles(c + 1))
+
+        w4_codes, w4_sc = mx_tiles("w4", H)
+        quantise_weight(w4_raw, w4_codes, w4_sc, ("scalar", "scalar"))
+
+        x = [work.tile([P, PN], F32, name=f"x{t}", tag="wide", bufs=4) for t in range(TILES)]
+        for lo, hi in STAGE2_CHUNKS:
+            for t in range(TILES):
+                nc.vector.tensor_tensor(
+                    x[t][:, lo:hi], page[t][:].indirect(entries(idx3, lo, hi)), aim_sb[t][:, lo:hi], ALU.subtract
+                )
+
+        x_codes, x_sc = mx_tiles("x", PN)
+
+        def quantise_x(lo):
+            words = psum.tile([P, per_chunk, 2, P], F32, name="words", tag="tr", bufs=3)
+            for b in range(per_chunk):
+                cols = slice(lo + b * P, lo + (b + 1) * P)
+                turned = psum.tile([P, H], F32, name="turned", tag="mm", bufs=5)
+                for t in range(TILES):
+                    nc.tensor.transpose(turned[:, t * P : (t + 1) * P], x[t][:, cols], ident[:])
+                rounded = work.tile([P, H], BF16, name="rounded", tag="h", bufs=6, align_bytes=64)
+                nc.scalar.copy(
+                    rounded[:].rearrange("j (u p e) -> j u p e", u=2, e=2),
+                    turned[:].rearrange("j (p u e) -> j u p e", u=2, e=2),
+                )
+                pairs = rounded[:].bitcast(F32)
+                for u in range(2):
+                    nc.tensor.transpose(words[:, b, u, :], pairs[:, u * P : (u + 1) * P], ident[:])
+            grouped = work.tile([P, CHUNK, PACK], BF16, name="grouped", tag="grouped", bufs=4, align_bytes=64)
+            nc.scalar.copy(
+                grouped[:].rearrange("p j i -> p (j i)").bitcast(F32).rearrange("p (b j u) -> p b j u", b=per_chunk, u=2),
+                words[:].rearrange("p b u j -> p b j u"),
+            )
+            cols = slice(lo, lo + CHUNK)
+            nc.vector.quantize_mx(
+                x_codes[:, cols].bitcast(FP8X4), x_sc[:, cols], grouped[:].rearrange("p j i -> p (j i)")
+            )
+
+        for lo, hi in STAGE2_CHUNKS:
+            for part in range(lo, hi, CHUNK):
+                quantise_x(part)
+            for t in range(TILES):
+                rows = slice(t * P, (t + 1) * P)
+                mixed = psum.tile([P, hi - lo], F32, name="mixed", tag="mm", bufs=5)
+                nc.tensor.matmul_mx(
+                    mixed[:], lhsT=w4_codes[:, rows].bitcast(FP8X4), lhsT_scale=w4_sc[:, rows],
+                    rhs=x_codes[:, lo:hi].bitcast(FP8X4), rhs_scale=x_sc[:, lo:hi], start=True, stop=True,
+                )
+                y = work.tile([P, hi - lo], F32, name="y", tag="bare", bufs=4)
+                nc.vector.tensor_tensor(y[:], mixed[:], x[t][:, lo:hi], ALU.mult)
+                nc.vector.tensor_tensor(ration[t][:].indirect(entries(idx4, lo, hi)), y[:], wgo_sb[:, lo:hi], ALU.mult)
+                if hi == PN:
+                    nc.sync.dma_start(out[rows, :], ration[t][:])

@@ -26,6 +26,8 @@ TILES = H // P
 CHUNK = 256
 STAGE2_CHUNKS = ((0, 256), (256, 512), (512, 1024))
 HALF = H // 2
+RING = 4
+STAGE1_STEPS = ((0, 0, 256), (0, 256, 512), (0, 512, 1024), (1, 0, 512), (1, 512, 1024))
 
 
 def tile_list_falcon_ration_features_kernel(
@@ -46,8 +48,9 @@ def tile_list_falcon_ration_features_kernel(
         def entries(idx, lo, hi):
             return idx[:, lo // 16 : hi // 16]
 
-        tab_sc = keep.tile([P, T], U8, name="tab_sc", align_bytes=64)
-        nc.vector.memset(tab_sc[:].bitcast(I32), 0)
+        tab_sc = [work.tile([P, T], U8, name=f"tab_sc{a}", tag="scales", bufs=2, align_bytes=64) for a in range(PASSES)]
+        for a in range(PASSES):
+            nc.vector.memset(tab_sc[a][:].bitcast(I32), 0)
         zero = keep.tile([P, 1], F32, name="zero")
         nc.vector.memset(zero[:], 0.0)
         zero_bias = keep.tile([P, 1], F32, name="zero_bias")
@@ -55,44 +58,63 @@ def tile_list_falcon_ration_features_kernel(
 
         w1_sc = keep.tile([P, PASSES, H], U8, name="w1_sc", align_bytes=64)
         nc.gpsimd.memset(w1_sc[:].rearrange("p a c -> p (a c)").bitcast(I32), 0)
-        v_sc_moved = keep.tile([P, S], U8, name="v_sc_moved", align_bytes=64)
-        nc.gpsimd.memset(v_sc_moved[:].bitcast(I32), 0)
         ident = keep.tile([P, P], F32, name="ident")
         make_identity(nc, ident[:])
 
         nc.sync.dma_start(idx1[:], offs)
-        tab = [keep.tile([P, T], I32, name=f"tab{a}") for a in range(PASSES)]
-        for a in range(PASSES):
-            nc.sync.dma_start(tab[a][:], tab_words[a].rearrange("p t i -> p (t i)").bitcast(I32))
-            if a == 0:
-                for q in range(4):
-                    nc.sync.dma_start(
-                        tab_sc[32 * q : 32 * q + 8, :].bitcast(I32), tab_scales[:, 4 * q : 4 * q + 4, :].bitcast(I32)
-                    )
+        tab = [work.tile([P, T], I32, name=f"tab{a}", tag="tab", bufs=2, align_bytes=64) for a in range(PASSES)]
 
-        def load_weight_pass(w, a):
-            raw = work.tile([P, PACK, H], F32, name="raw", tag="raw", bufs=4)
-            nc.sync.dma_start(raw[:], w[a * K_PASS : (a + 1) * K_PASS, :].rearrange("(p i) c -> p i c", i=PACK))
+        def load_table_pass(a):
+            nc.sync.dma_start(tab[a][:], tab_words[a].rearrange("p t i -> p (t i)").bitcast(I32))
+
+        def load_weight(w, a, half):
+            raw = work.tile([P, PACK, HALF], F32, name="raw", tag="raw", bufs=4)
+            rows = w[a * K_PASS : (a + 1) * K_PASS, half * HALF : (half + 1) * HALF]
+            nc.sync.dma_start(raw[:], rows.rearrange("(p i) c -> p i c", i=PACK))
             return raw
 
-        w2_raw = [load_weight_pass(w2, a) for a in range(PASSES)]
+        def load_rows(name, src, t):
+            rows = keep.tile([P, src.shape[1]], F32, name=f"{name}{t}")
+            nc.sync.dma_start(rows[:], src[t * P : (t + 1) * P, :])
+            return rows
+
+        def load_table_scales(a):
+            for q in range(4):
+                nc.sync.dma_start(
+                    tab_sc[a][32 * q : 32 * q + 4, :].bitcast(I32), tab_scales[a, 4 * q : 4 * q + 4, :].bitcast(I32)
+                )
+
+        load_table_pass(0)
+        load_table_scales(0)
+        w2_raw = [[load_weight(w2, a, 0) for a in range(PASSES)]]
+        load_table_scales(1)
+        load_table_pass(1)
         w1_codes = keep.tile([P, PASSES, 2 * H], U8, name="w1_codes", align_bytes=64)
         nc.sync.dma_start(w1_codes[:].bitcast(I32), w1_words.rearrange("a p c -> p a c").bitcast(I32))
-        picked_sc = keep.tile([P, S], U8, name="picked_sc", align_bytes=64)
-        nc.vector.tensor_copy(picked_sc[:], tab_sc[:].indirect(idx1[:]))
-        for q in range(4):
-            nc.sync.dma_start(
-                v_sc_moved[32 * q : 32 * q + 4, :].bitcast(I32), picked_sc[32 * q + 4 : 32 * q + 8, :].bitcast(I32)
-            )
-        w3_raw = [load_weight_pass(w3, a) for a in range(PASSES)]
+        w3_raw = [[load_weight(w3, a, 0) for a in range(PASSES)]]
+
+        v = [keep.tile([P, S], U32, name=f"v{a}", align_bytes=64) for a in range(PASSES)]
+        nc.vector.tensor_copy(v[0][:], tab[0][:].bitcast(U32).indirect(idx1[:]))
+        v_sc = [keep.tile([P, S], U8, name=f"v_sc{a}", align_bytes=64) for a in range(PASSES)]
+        for a in range(PASSES):
+            nc.vector.tensor_copy(v_sc[a][:], tab_sc[a][:].indirect(idx1[:]))
+
         nc.sync.dma_start(idx2[:], offs2)
-        wgs_sb = keep.tile([P, S], F32, name="wgs_sb")
-        nc.sync.dma_start(wgs_sb[:], wgs)
-        page = [keep.tile([P, T2], F32, name=f"page{t}") for t in range(TILES)]
-        for t in range(TILES):
-            nc.sync.dma_start(page[t][:], page0[t * P : (t + 1) * P, :])
+        wgs_sb = load_rows("wgs_sb", wgs, 0)
+        page = [load_rows("states", page0, t) for t in range(2)]
+        w2_raw.append([load_weight(w2, a, 1) for a in range(PASSES)])
+        w3_raw.append([load_weight(w3, a, 1) for a in range(PASSES)])
         nc.sync.dma_start(idx3[:], offs3)
+        aim_sb = [load_rows("aims", aim, t) for t in range(2)]
+        page.extend([load_rows("states", page0, t) for t in range(2, TILES)])
+        for t in range(2, TILES):
+            late_aim = work.tile([P, PN], F32, name="late_aim", tag="scales", bufs=2, align_bytes=64)
+            nc.sync.dma_start(late_aim[:], aim[t * P : (t + 1) * P, :])
+            aim_sb.append(late_aim)
+        w4_raw = [load_weight(w4, 0, half) for half in range(2)]
+        wgo_sb = load_rows("wgo_sb", wgo, 0)
         nc.sync.dma_start(idx4[:], offs4)
+        ration = [load_rows("ration", page1, t) for t in range(TILES)]
 
         for q in range(4):
             nc.gpsimd.dma_start(
@@ -105,137 +127,178 @@ def tile_list_falcon_ration_features_kernel(
         neg_gain = keep.tile([P, TILES], F32, name="neg_gain")
         nc.gpsimd.tensor_scalar(neg_gain[:], gain_sb[:], -1.0, 0.0, ALU.mult, ALU.add)
 
-        v = [keep.tile([P, S], U32, name=f"v{a}", align_bytes=64) for a in range(PASSES)]
-        for a in range(PASSES):
-            nc.vector.tensor_copy(v[a][:], tab[a][:].bitcast(U32).indirect(idx1[:]))
+        def quantise_weight(raw, codes, scales, copy, grouped):
+            copy(grouped.rearrange("p (c e i) -> p c i e", e=4, i=PACK), raw[:].rearrange("p i (c e) -> p c i e", e=4))
+            nc.vector.quantize_mx(codes.bitcast(FP8X4), scales, grouped)
 
-        def quantise_weight(raw, codes, scales, engines):
-            for half in range(2):
-                cols = slice(half * HALF, (half + 1) * HALF)
-                grouped = work.tile([P, HALF, PACK], BF16, name="grouped", tag="grouped", bufs=4, align_bytes=64)
-                dst = grouped[:].rearrange("p (c e) i -> p c i e", e=4)
-                src = raw[:, :, cols].rearrange("p i (c e) -> p c i e", e=4)
-                if engines[half] == "vector":
-                    nc.vector.tensor_copy(dst, src)
-                else:
-                    nc.scalar.copy(dst, src)
-                nc.vector.quantize_mx(
-                    codes[:, cols].bitcast(FP8X4), scales[:, cols], grouped[:].rearrange("p c i -> p (c i)")
-                )
+        def fresh_staging():
+            grouped = work.tile([P, HALF * PACK], BF16, name="grouped", tag="grouped", bufs=4, align_bytes=64)
+            return grouped[:]
+
+        waves = [keep.tile([P, H], F32, name=f"wave{i}", align_bytes=64) for i in range(RING)]
+        bares = [keep.tile([P, H], F32, name=f"bare{i}", align_bytes=64) for i in range(RING)]
+
+        def staging_behind(n):
+            return (waves[n % RING][:].bitcast(BF16), bares[n % RING][:].bitcast(BF16))
 
         def mx_tiles(name, width):
             codes = keep.tile([P, width], U32, name=name + "_codes", align_bytes=64)
             scales = keep.tile([P, width], U8, name=name + "_sc", align_bytes=64)
             return codes, scales
 
-        w2_q = [mx_tiles(f"w2_{a}", H) for a in range(PASSES)]
-        w3_q = [mx_tiles(f"w3_{a}", H) for a in range(PASSES)]
-        for a in range(PASSES):
-            quantise_weight(w2_raw[a], w2_q[a][0], w2_q[a][1], ("vector", "scalar"))
+        def quantise_half(name, raws, copies, staging):
+            made = []
+            for a in range(PASSES):
+                codes, scales = mx_tiles(f"{name}_{a}", HALF)
+                quantise_weight(raws[a], codes[:], scales[:], copies[a], staging[a])
+                made.append((codes[:].bitcast(FP8X4), scales[:]))
+            return made
 
-        v_sc_packed = [picked_sc[4 * a : P, :] for a in range(PASSES)]
-        v_sc_plain = [picked_sc[:], v_sc_moved[:]]
-
-        def first_product(jb, moving, v_sc):
-            bank = psum.tile([P, H], F32, name="bank", tag="mm", bufs=5)
+        def first_product(sums, jb, moving):
             cols = slice(jb * P, (jb + 1) * P)
             for a in range(PASSES):
                 codes, scales = moving[a]
                 nc.tensor.matmul_mx(
-                    bank[:], lhsT=v[a][:, cols].bitcast(FP8X4), lhsT_scale=v_sc[a][:, cols],
+                    sums, lhsT=v[a][:, cols].bitcast(FP8X4), lhsT_scale=v_sc[a][:, cols],
                     rhs=codes, rhs_scale=scales, start=(a == 0), stop=(a == PASSES - 1),
                 )
-            return bank
-
-        w1_mv = [(w1_codes[:, a, :].bitcast(FP4X4), w1_sc[:, a, :]) for a in range(PASSES)]
-        w2_mv = [(w2_q[a][0][:].bitcast(FP8X4), w2_q[a][1][:]) for a in range(PASSES)]
-        w3_mv = [(w3_q[a][0][:].bitcast(FP8X4), w3_q[a][1][:]) for a in range(PASSES)]
-
-        def reduced_angle(jb, angle):
-            bank = first_product(jb, w2_mv, v_sc_packed)
-            turns = work.tile([P, H], I32, name="turns", tag="turns", bufs=2)
-            nc.vector.tensor_scalar(turns[:], bank[:], 1.0 / (2.0 * math.pi), None, ALU.mult)
-            nc.vector.scalar_tensor_tensor(angle, turns[:], -2.0 * math.pi, bank[:], ALU.mult, ALU.add)
 
         per_chunk = CHUNK // P
+        chunks = S // CHUNK
 
-        def reduced_angles(c):
-            both = work.tile([P, per_chunk, H], F32, name="angles", tag="wide", bufs=4)
+        def half_product(c, moving, tag, bufs):
+            bank = psum.tile([P, per_chunk, HALF], F32, name="bank", tag=tag, bufs=bufs)
             for b in range(per_chunk):
-                reduced_angle(c * per_chunk + b, both[:, b, :])
-            return both
+                first_product(bank[:, b, :], c * per_chunk + b, moving)
+            return bank[:].rearrange("j b r -> j (b r)")
 
-        angles = [reduced_angles(0)]
-        quantise_weight(w3_raw[0], w3_q[0][0], w3_q[0][1], ("scalar", "scalar"))
-        quantise_weight(w3_raw[1], w3_q[1][0], w3_q[1][1], ("vector", "scalar"))
+        w1_mv = [(w1_codes[:, a, :].bitcast(FP4X4), w1_sc[:, a, :]) for a in range(PASSES)]
+        w2_mv = [quantise_half("w2a", w2_raw[0], (nc.scalar.copy, nc.scalar.copy), (fresh_staging(), fresh_staging()))]
+        for lo in range(0, S, S // 2):
+            nc.vector.tensor_copy(
+                v[1][:, lo : lo + S // 2], tab[1][:].bitcast(U32).indirect(entries(idx1, lo, lo + S // 2))
+            )
+        w3_mv = [quantise_half("w3a", w3_raw[0], (nc.vector.tensor_copy, nc.scalar.copy), (fresh_staging(), fresh_staging()))]
 
-        aim_sb = []
-        for pair in range(TILES // 2):
-            aim_pair = work.tile([P, 2, PN], F32, name="aim_pair", tag="raw", bufs=4)
-            nc.sync.dma_start(aim_pair[:], aim[2 * pair * P : (2 * pair + 2) * P, :].rearrange("(t p) j -> p t j", p=P))
-            aim_sb.extend([aim_pair[:, 0, :], aim_pair[:, 1, :]])
-        w4_raw = load_weight_pass(w4, 0)
-        wgo_sb = keep.tile([P, PN], F32, name="wgo_sb")
-        nc.sync.dma_start(wgo_sb[:], wgo)
-        ration = [keep.tile([P, T2], F32, name=f"ration{t}") for t in range(TILES)]
-        for t in range(TILES):
-            nc.sync.dma_start(ration[t][:], page1[t * P : (t + 1) * P, :])
+        angle_tiles = {}
 
-        for c in range(S // CHUNK):
-            terms = []
-            for b in range(per_chunk):
-                jb = c * per_chunk + b
-                bank = first_product(jb, w1_mv, v_sc_plain)
-                bounded = work.tile([P, H], F32, name="bounded", tag="bounded", bufs=4)
-                nc.scalar.activation(bounded[:], bank[:], ACT.Tanh, bias=zero_bias[:], scale=-1.0)
-                wave = work.tile([P, H], F32, name="wave", tag="wave", bufs=4)
-                nc.scalar.activation(wave[:], angles[c][:, b, :], ACT.Sin, bias=zero_bias[:], scale=0.5)
-                nc.scalar.activation(wave[:], wave[:], ACT.Square, bias=zero_bias[:], scale=math.sqrt(2.0))
-                bank = first_product(jb, w3_mv, v_sc_packed)
-                bare = work.tile([P, H], F32, name="bare", tag="bare", bufs=4)
-                nc.scalar.activation(bare[:], bank[:], ACT.Copy, bias=-1.0, scale=-1.0)
-                terms.append((bounded, wave, bare))
-            for t in range(TILES):
-                rows = slice(t * P, (t + 1) * P)
-                total = psum.tile([P, CHUNK], F32, name="total", tag="tr", bufs=3)
-                for b in range(per_chunk):
-                    for n, term in enumerate(terms[b]):
-                        nc.tensor.matmul(
-                            total[:, b * P : (b + 1) * P], lhsT=term[:, rows], rhs=ident[:],
-                            is_transpose=True, start=(n == 0), stop=(n == 2),
-                        )
-                h = work.tile([P, CHUNK], F32, name="h", tag="h", bufs=6, align_bytes=64)
-                nc.scalar.activation(h[:], total[:], ACT.Copy, scale=neg_gain[:, t : t + 1])
-                lo, hi = c * CHUNK, (c + 1) * CHUNK
-                nc.vector.tensor_tensor(page[t][:].indirect(entries(idx2, lo, hi)), h[:], wgs_sb[:, lo:hi], ALU.mult)
-            if c + 1 < S // CHUNK:
-                angles.append(reduced_angles(c + 1))
+        def reduce_angles(half, c):
+            if c % 2 == 0:
+                angle_tiles[(half, c // 2)] = work.tile([P, 2, H], F32, name="angles", tag="wide", bufs=4)
+            angle = angle_tiles[(half, c // 2)][:, c % 2, :]
+            bank = half_product(c, w2_mv[half], "angle", 2)
+            turns = work.tile([P, H], I32, name="turns", tag="turns", bufs=2)
+            nc.vector.tensor_scalar(turns[:], bank, 1.0 / (2.0 * math.pi), None, ALU.mult)
+            nc.vector.scalar_tensor_tensor(angle, turns[:], -2.0 * math.pi, bank, ALU.mult, ALU.add)
+            return angle
+
+        bounded = []
+
+        def bound(jb):
+            bank = psum.tile([P, H], F32, name="bank", tag="mm", bufs=3)
+            first_product(bank[:], jb, w1_mv)
+            term = keep.tile([P, H], F32, name=f"bounded{jb}")
+            nc.scalar.activation(term[:], bank[:], ACT.Tanh, bias=zero_bias[:], scale=-1.0)
+            bounded.append(term)
+
+        x = {}
+
+        def recall(t, lo, hi):
+            if lo == 0:
+                x[t] = work.tile([P, PN], F32, name=f"x{t}", tag="wide", bufs=4)
+            nc.vector.tensor_tensor(
+                x[t][:, lo:hi], page[t][:].indirect(entries(idx3, lo, hi)), aim_sb[t][:, lo:hi], ALU.subtract
+            )
 
         w4_codes, w4_sc = mx_tiles("w4", H)
-        quantise_weight(w4_raw, w4_codes, w4_sc, ("scalar", "scalar"))
+        rounded = work.tile([P, PN // P, H], BF16, name="rounded", tag="tab", bufs=2, align_bytes=64)
 
-        x = [work.tile([P, PN], F32, name=f"x{t}", tag="wide", bufs=4) for t in range(TILES)]
-        for lo, hi in STAGE2_CHUNKS:
-            for t in range(TILES):
-                nc.vector.tensor_tensor(
-                    x[t][:, lo:hi], page[t][:].indirect(entries(idx3, lo, hi)), aim_sb[t][:, lo:hi], ALU.subtract
-                )
+        def round_x(half, c):
+            turned = psum.tile([P, per_chunk, HALF], F32, name="turned", tag="mm", bufs=3)
+            for b in range(per_chunk):
+                jb = c * per_chunk + b
+                for inner in range(2):
+                    nc.tensor.transpose(
+                        turned[:, b, inner * P : (inner + 1) * P], x[2 * half + inner][:, jb * P : (jb + 1) * P], ident[:]
+                    )
+            blocks = rounded[:, c * per_chunk : (c + 1) * per_chunk, :]
+            nc.scalar.copy(
+                blocks.rearrange("j b (u h p e) -> j b u h p e", u=2, h=2, e=2)[:, :, :, half, :, :],
+                turned[:].rearrange("j b (p u e) -> j b u p e", u=2, e=2),
+            )
 
-        x_codes, x_sc = mx_tiles("x", PN)
+        def weigh_x(t, lo, hi):
+            nc.gpsimd.tensor_tensor(aim_sb[t][:, lo:hi], x[t][:, lo:hi], wgo_sb[:, lo:hi], ALU.mult)
+
+        units = [(half, c) for half in range(2) for c in range(chunks)]
+        angles = [reduce_angles(0, 0)]
+
+        def make_terms(n):
+            half, c = units[n]
+            if half == 0:
+                for b in range(per_chunk):
+                    bound(c * per_chunk + b)
+            wave = waves[n % RING][:]
+            nc.scalar.activation(wave, angles[n], ACT.Sin, bias=zero_bias[:], scale=0.5)
+            nc.scalar.activation(wave, wave, ACT.Square, bias=zero_bias[:], scale=math.sqrt(2.0))
+            bank = half_product(c, w3_mv[half], "mm", 3)
+            nc.scalar.activation(bares[n % RING][:], bank, ACT.Copy, bias=-1.0, scale=-1.0)
+            if n + 1 < len(units):
+                angles.append(reduce_angles(*units[n + 1]))
+
+        for step, (half, lo, hi) in enumerate(STAGE1_STEPS):
+            for c in range(lo // CHUNK, hi // CHUNK):
+                make_terms(half * chunks + c)
+            for inner in range(2):
+                t = 2 * half + inner
+                total = psum.tile([P, hi - lo], F32, name="total", tag="tr", bufs=3)
+                for jb in range(lo // P, hi // P):
+                    slot = (half * chunks + jb // per_chunk) % RING
+                    first = jb % per_chunk * HALF + inner * P
+                    terms = (
+                        bounded[jb][:, t * P : (t + 1) * P],
+                        waves[slot][:, first : first + P],
+                        bares[slot][:, first : first + P],
+                    )
+                    for m, term in enumerate(terms):
+                        nc.tensor.matmul(
+                            total[:, jb * P - lo : (jb + 1) * P - lo], lhsT=term, rhs=ident[:],
+                            is_transpose=True, start=(m == 0), stop=(m == 2),
+                        )
+                h = work.tile([P, hi - lo], F32, name="h", tag="h", bufs=4, align_bytes=64)
+                nc.scalar.activation(h[:], total[:], ACT.Copy, scale=neg_gain[:, t : t + 1])
+                n = step
+                nc.gpsimd.tensor_tensor(h[:], h[:], wgs_sb[:, lo:hi], ALU.mult)
+                nc.vector.tensor_copy(page[t][:].indirect(entries(idx2, lo, hi)), h[:])
+            if step == 0:
+                w2_mv.append(quantise_half("w2b", w2_raw[1], (nc.scalar.copy, nc.scalar.copy), staging_behind(0)))
+            if step == 1:
+                w3_mv.append(quantise_half("w3b", w3_raw[1], (nc.scalar.copy, nc.scalar.copy), staging_behind(1)))
+            if step == 2:
+                for t in range(2):
+                    recall(t, 0, PN)
+            if step == 3:
+                for part in range(2):
+                    cols = slice(part * HALF, (part + 1) * HALF)
+                    quantise_weight(w4_raw[part], w4_codes[:, cols], w4_sc[:, cols], nc.scalar.copy, staging_behind(1)[part])
+            if half == 1:
+                for c in range(lo // CHUNK, hi // CHUNK):
+                    round_x(0, c)
+                for t in range(2):
+                    weigh_x(t, lo, hi)
+
+        for lo, hi in ((0, CHUNK), (CHUNK, PN)):
+            for t in range(2, TILES):
+                recall(t, lo, hi)
+
+        x_codes = work.tile([P, PN], U32, name="x_codes", tag="tab", bufs=2, align_bytes=64)
+        x_sc = keep.tile([P, PN], U8, name="x_sc", align_bytes=64)
 
         def quantise_x(lo):
             words = psum.tile([P, per_chunk, 2, P], F32, name="words", tag="tr", bufs=3)
+            round_x(1, lo // CHUNK)
             for b in range(per_chunk):
-                cols = slice(lo + b * P, lo + (b + 1) * P)
-                turned = psum.tile([P, H], F32, name="turned", tag="mm", bufs=5)
-                for t in range(TILES):
-                    nc.tensor.transpose(turned[:, t * P : (t + 1) * P], x[t][:, cols], ident[:])
-                rounded = work.tile([P, H], BF16, name="rounded", tag="h", bufs=6, align_bytes=64)
-                nc.scalar.copy(
-                    rounded[:].rearrange("j (u p e) -> j u p e", u=2, e=2),
-                    turned[:].rearrange("j (p u e) -> j u p e", u=2, e=2),
-                )
-                pairs = rounded[:].bitcast(F32)
+                pairs = rounded[:, lo // P + b, :].bitcast(F32)
                 for u in range(2):
                     nc.tensor.transpose(words[:, b, u, :], pairs[:, u * P : (u + 1) * P], ident[:])
             grouped = work.tile([P, CHUNK, PACK], BF16, name="grouped", tag="grouped", bufs=4, align_bytes=64)
@@ -248,18 +311,33 @@ def tile_list_falcon_ration_features_kernel(
                 x_codes[:, cols].bitcast(FP8X4), x_sc[:, cols], grouped[:].rearrange("p j i -> p (j i)")
             )
 
+        def mix(t, lo, hi):
+            rows = slice(t * P, (t + 1) * P)
+            mixed = psum.tile([P, hi - lo], F32, name="mixed", tag="mm", bufs=3)
+            nc.tensor.matmul_mx(
+                mixed[:], lhsT=w4_codes[:, rows].bitcast(FP8X4), lhsT_scale=w4_sc[:, rows],
+                rhs=x_codes[:, lo:hi].bitcast(FP8X4), rhs_scale=x_sc[:, lo:hi], start=True, stop=True,
+            )
+            y = bounded[(lo // CHUNK % 2) * TILES + t][:, : hi - lo]
+            nc.scalar.copy(y, mixed[:])
+            if t >= 2:
+                weigh_x(t, lo, hi)
+            nc.gpsimd.tensor_tensor(y, y, aim_sb[t][:, lo:hi], ALU.mult)
+            return y
+
+        def place(t, lo, hi, y):
+            nc.vector.tensor_copy(ration[t][:].indirect(entries(idx4, lo, hi)), y)
+            if hi == PN:
+                nc.sync.dma_start(out[t * P : (t + 1) * P, :], ration[t][:])
+
         for lo, hi in STAGE2_CHUNKS:
             for part in range(lo, hi, CHUNK):
                 quantise_x(part)
-            for t in range(TILES):
-                rows = slice(t * P, (t + 1) * P)
-                mixed = psum.tile([P, hi - lo], F32, name="mixed", tag="mm", bufs=5)
-                nc.tensor.matmul_mx(
-                    mixed[:], lhsT=w4_codes[:, rows].bitcast(FP8X4), lhsT_scale=w4_sc[:, rows],
-                    rhs=x_codes[:, lo:hi].bitcast(FP8X4), rhs_scale=x_sc[:, lo:hi], start=True, stop=True,
-                )
-                y = work.tile([P, hi - lo], F32, name="y", tag="bare", bufs=4)
-                nc.vector.tensor_tensor(y[:], mixed[:], x[t][:, lo:hi], ALU.mult)
-                nc.vector.tensor_tensor(ration[t][:].indirect(entries(idx4, lo, hi)), y[:], wgo_sb[:, lo:hi], ALU.mult)
-                if hi == PN:
-                    nc.sync.dma_start(out[rows, :], ration[t][:])
+            ys = []
+            for t in range(TILES + 1):
+                if t > 0:
+                    ys_t = t - 1
+                if t < TILES:
+                    ys.append(mix(t, lo, hi))
+                if t > 0:
+                    place(ys_t, lo, hi, ys[ys_t])

@@ -27,7 +27,8 @@ CHUNK = 256
 STAGE2_CHUNKS = ((0, 256), (256, 512), (512, 1024))
 HALF = H // 2
 RING = 4
-STAGE1_STEPS = ((0, 0, 256), (0, 256, 512), (0, 512, 1024), (1, 0, 512), (1, 512, 1024))
+BANK = 512
+STAGE1_STEPS = ((0, 0, 256), (0, 256, 512), (0, 512, 768), (0, 768, 1024), (1, 0, 256), (1, 256, 512), (1, 512, 1024))
 
 
 def tile_list_falcon_ration_features_kernel(
@@ -62,7 +63,8 @@ def tile_list_falcon_ration_features_kernel(
         make_identity(nc, ident[:])
 
         nc.sync.dma_start(idx1[:], offs)
-        tab = [work.tile([P, T], I32, name=f"tab{a}", tag="tab", bufs=2, align_bytes=64) for a in range(PASSES)]
+        tab = [work.tile([P, T], I32, name=f"tab{a}", tag=f"tab{a}", align_bytes=64) for a in range(PASSES)]
+        banks = [psum.tile([P, BANK], F32, name=f"bank{i}") for i in range(8)]
 
         def load_table_pass(a):
             nc.sync.dma_start(tab[a][:], tab_words[a].rearrange("p t i -> p (t i)").bitcast(I32))
@@ -138,8 +140,6 @@ def tile_list_falcon_ration_features_kernel(
         waves = [keep.tile([P, H], F32, name=f"wave{i}", align_bytes=64) for i in range(RING)]
         bares = [keep.tile([P, H], F32, name=f"bare{i}", align_bytes=64) for i in range(RING)]
 
-        def staging_behind(n):
-            return (waves[n % RING][:].bitcast(BF16), bares[n % RING][:].bitcast(BF16))
 
         def mx_tiles(name, width):
             codes = keep.tile([P, width], U32, name=name + "_codes", align_bytes=64)
@@ -166,178 +166,179 @@ def tile_list_falcon_ration_features_kernel(
         per_chunk = CHUNK // P
         chunks = S // CHUNK
 
-        def half_product(c, moving, tag, bufs):
-            bank = psum.tile([P, per_chunk, HALF], F32, name="bank", tag=tag, bufs=bufs)
+        def half_product(bank, c, moving):
             for b in range(per_chunk):
-                first_product(bank[:, b, :], c * per_chunk + b, moving)
-            return bank[:].rearrange("j b r -> j (b r)")
+                first_product(bank[:, b * HALF : (b + 1) * HALF], c * per_chunk + b, moving)
 
+        on_scalar = (nc.scalar.copy, nc.scalar.copy)
         w1_mv = [(w1_codes[:, a, :].bitcast(FP4X4), w1_sc[:, a, :]) for a in range(PASSES)]
-        w2_mv = [quantise_half("w2a", w2_raw[0], (nc.scalar.copy, nc.scalar.copy), (fresh_staging(), fresh_staging()))]
+        w2_mv = [quantise_half("w2a", w2_raw[0], on_scalar, (fresh_staging(), fresh_staging()))]
         for lo in range(0, S, S // 2):
             nc.vector.tensor_copy(
                 v[1][:, lo : lo + S // 2], tab[1][:].bitcast(U32).indirect(entries(idx1, lo, lo + S // 2))
             )
         w3_mv = [quantise_half("w3a", w3_raw[0], (nc.vector.tensor_copy, nc.scalar.copy), (fresh_staging(), fresh_staging()))]
 
-        angle_tiles = {}
+        x = [keep.tile([P, PN], F32, name=f"x{t}") for t in range(TILES)]
+        turns_ring = [keep.tile([P, H], I32, name=f"turns{i}") for i in range(2)]
 
-        def reduce_angles(half, c):
-            if c % 2 == 0:
-                angle_tiles[(half, c // 2)] = work.tile([P, 2, H], F32, name="angles", tag="wide", bufs=4)
-            angle = angle_tiles[(half, c // 2)][:, c % 2, :]
-            bank = half_product(c, w2_mv[half], "angle", 2)
-            turns = work.tile([P, H], I32, name="turns", tag="turns", bufs=2)
-            nc.vector.tensor_scalar(turns[:], bank, 1.0 / (2.0 * math.pi), None, ALU.mult)
-            nc.vector.scalar_tensor_tensor(angle, turns[:], -2.0 * math.pi, bank, ALU.mult, ALU.add)
-            return angle
+        def angle_of(n):
+            return x[n // 2][:, n % 2 * H : (n % 2 + 1) * H]
 
-        bounded = []
+        def reduce_angles(n):
+            half, c = divmod(n, chunks)
+            bank = banks[n % 2]
+            half_product(bank, c, w2_mv[half])
+            if n // 2 == 2:
+                turns = x[1][:, n % 2 * H : (n % 2 + 1) * H].bitcast(I32)
+            else:
+                turns = turns_ring[n % 2][:]
+            if n >= 6:
+                nc.scalar.activation(angle_of(n), bank[:], ACT.Abs, bias=zero_bias[:])
+                nc.scalar.activation(turns.bitcast(U32), angle_of(n), ACT.Copy, bias=0.25, scale=1.0 / (2.0 * math.pi))
+                nc.vector.scalar_tensor_tensor(angle_of(n), turns, -2.0 * math.pi, angle_of(n), ALU.mult, ALU.add)
+            else:
+                nc.vector.tensor_scalar(turns, bank[:], 1.0 / (2.0 * math.pi), None, ALU.mult)
+                nc.vector.scalar_tensor_tensor(angle_of(n), turns, -2.0 * math.pi, bank[:], ALU.mult, ALU.add)
+
+        bounded = [keep.tile([P, H], F32, name=f"bounded{jb}") for jb in range(S // P)]
 
         def bound(jb):
-            bank = psum.tile([P, H], F32, name="bank", tag="mm", bufs=3)
+            bank = banks[2 + jb % 2]
             first_product(bank[:], jb, w1_mv)
-            term = keep.tile([P, H], F32, name=f"bounded{jb}")
-            nc.scalar.activation(term[:], bank[:], ACT.Tanh, bias=zero_bias[:], scale=-1.0)
-            bounded.append(term)
-
-        x = {}
-
-        def recall(t, lo, hi):
-            if lo == 0:
-                x[t] = work.tile([P, PN], F32, name=f"x{t}", tag="wide", bufs=4)
-            nc.vector.tensor_tensor(
-                x[t][:, lo:hi], page[t][:].indirect(entries(idx3, lo, hi)), aim_sb[t][:, lo:hi], ALU.subtract
-            )
-
-        w4_codes, w4_sc = mx_tiles("w4", H)
-        rounded = work.tile([P, PN // P, H], BF16, name="rounded", tag="tab", bufs=2, align_bytes=64)
-
-        def round_x(half, c):
-            turned = psum.tile([P, per_chunk, HALF], F32, name="turned", tag="mm", bufs=3)
-            for b in range(per_chunk):
-                jb = c * per_chunk + b
-                for inner in range(2):
-                    nc.tensor.transpose(
-                        turned[:, b, inner * P : (inner + 1) * P], x[2 * half + inner][:, jb * P : (jb + 1) * P], ident[:]
-                    )
-            blocks = rounded[:, c * per_chunk : (c + 1) * per_chunk, :]
-            nc.scalar.copy(
-                blocks.rearrange("j b (u h p e) -> j b u h p e", u=2, h=2, e=2)[:, :, :, half, :, :],
-                turned[:].rearrange("j b (p u e) -> j b u p e", u=2, e=2),
-            )
-
-        def weigh_x(t, lo, hi):
-            nc.gpsimd.tensor_tensor(aim_sb[t][:, lo:hi], x[t][:, lo:hi], wgo_sb[:, lo:hi], ALU.mult)
-
-        units = [(half, c) for half in range(2) for c in range(chunks)]
-        angles = [reduce_angles(0, 0)]
+            nc.scalar.activation(bounded[jb][:], bank[:], ACT.Tanh, bias=zero_bias[:], scale=-1.0)
 
         def make_terms(n):
-            half, c = units[n]
+            half, c = divmod(n, chunks)
             if half == 0:
                 for b in range(per_chunk):
                     bound(c * per_chunk + b)
             wave = waves[n % RING][:]
-            nc.scalar.activation(wave, angles[n], ACT.Sin, bias=zero_bias[:], scale=0.5)
+            nc.scalar.activation(wave, angle_of(n), ACT.Sin, bias=zero_bias[:], scale=0.5)
             nc.scalar.activation(wave, wave, ACT.Square, bias=zero_bias[:], scale=math.sqrt(2.0))
-            bank = half_product(c, w3_mv[half], "mm", 3)
-            nc.scalar.activation(bares[n % RING][:], bank, ACT.Copy, bias=-1.0, scale=-1.0)
-            if n + 1 < len(units):
-                angles.append(reduce_angles(*units[n + 1]))
+            bank = banks[4] if half == 0 else banks[3 + n % 2]
+            half_product(bank, c, w3_mv[half])
+            nc.scalar.activation(bares[n % RING][:], bank[:], ACT.Copy, bias=-1.0, scale=-1.0)
 
-        for step, (half, lo, hi) in enumerate(STAGE1_STEPS):
-            for c in range(lo // CHUNK, hi // CHUNK):
-                make_terms(half * chunks + c)
-            for inner in range(2):
-                t = 2 * half + inner
-                total = psum.tile([P, hi - lo], F32, name="total", tag="tr", bufs=3)
-                for jb in range(lo // P, hi // P):
-                    slot = (half * chunks + jb // per_chunk) % RING
-                    first = jb % per_chunk * HALF + inner * P
-                    terms = (
-                        bounded[jb][:, t * P : (t + 1) * P],
-                        waves[slot][:, first : first + P],
-                        bares[slot][:, first : first + P],
+        h_ring = [keep.tile([P, 2 * CHUNK], F32, name=f"h{i}") for i in range(RING)]
+
+        def renew(step, inner):
+            half, lo, hi = STAGE1_STEPS[step]
+            t = 2 * half + inner
+            total = banks[5 + (2 * step + inner) % 3]
+            for jb in range(lo // P, hi // P):
+                slot = (half * chunks + jb // per_chunk) % RING
+                first = jb % per_chunk * HALF + inner * P
+                terms = (
+                    bounded[jb][:, t * P : (t + 1) * P],
+                    waves[slot][:, first : first + P],
+                    bares[slot][:, first : first + P],
+                )
+                for m, term in enumerate(terms):
+                    nc.tensor.matmul(
+                        total[:, jb * P - lo : (jb + 1) * P - lo], lhsT=term, rhs=ident[:],
+                        is_transpose=True, start=(m == 0), stop=(m == 2),
                     )
-                    for m, term in enumerate(terms):
-                        nc.tensor.matmul(
-                            total[:, jb * P - lo : (jb + 1) * P - lo], lhsT=term, rhs=ident[:],
-                            is_transpose=True, start=(m == 0), stop=(m == 2),
-                        )
-                h = work.tile([P, hi - lo], F32, name="h", tag="h", bufs=4, align_bytes=64)
-                nc.scalar.activation(h[:], total[:], ACT.Copy, scale=neg_gain[:, t : t + 1])
-                n = step
-                nc.gpsimd.tensor_tensor(h[:], h[:], wgs_sb[:, lo:hi], ALU.mult)
-                nc.vector.tensor_copy(page[t][:].indirect(entries(idx2, lo, hi)), h[:])
-            if step == 0:
-                w2_mv.append(quantise_half("w2b", w2_raw[1], (nc.scalar.copy, nc.scalar.copy), staging_behind(0)))
-            if step == 1:
-                w3_mv.append(quantise_half("w3b", w3_raw[1], (nc.scalar.copy, nc.scalar.copy), staging_behind(1)))
-            if step == 2:
-                for t in range(2):
-                    recall(t, 0, PN)
-            if step == 3:
-                for part in range(2):
-                    cols = slice(part * HALF, (part + 1) * HALF)
-                    quantise_weight(w4_raw[part], w4_codes[:, cols], w4_sc[:, cols], nc.scalar.copy, staging_behind(1)[part])
-            if half == 1:
-                for c in range(lo // CHUNK, hi // CHUNK):
-                    round_x(0, c)
-                for t in range(2):
-                    weigh_x(t, lo, hi)
+            h = h_ring[(2 * step + inner) % RING][:, : hi - lo]
+            nc.scalar.activation(h, total[:, : hi - lo], ACT.Copy, scale=neg_gain[:, t : t + 1])
+            nc.vector.tensor_tensor(page[t][:].indirect(entries(idx2, lo, hi)), h, wgs_sb[:, lo:hi], ALU.mult)
+
+        def recall(t, lo, hi):
+            nc.vector.tensor_tensor(
+                x[t][:, lo:hi], page[t][:].indirect(entries(idx3, lo, hi)), aim_sb[t][:, lo:hi], ALU.subtract
+            )
+
+        rounded = work.tile([P, PN // P, H], BF16, name="rounded", tag="tab0", align_bytes=64)
+
+        def round_x(turned, half, c):
+            for b in range(per_chunk):
+                jb = c * per_chunk + b
+                for inner in range(2):
+                    first = b * HALF + inner * P
+                    nc.tensor.transpose(
+                        turned[:, first : first + P], x[2 * half + inner][:, jb * P : (jb + 1) * P], ident[:]
+                    )
+            blocks = rounded[:, c * per_chunk : (c + 1) * per_chunk, :]
+            nc.scalar.copy(
+                blocks.rearrange("j b (u h p e) -> j b u h p e", u=2, h=2, e=2)[:, :, :, half, :, :],
+                turned[:].rearrange("j (b p u e) -> j b u p e", b=per_chunk, u=2, e=2),
+            )
+
+        reduce_angles(0)
+        for step in range(chunks):
+            make_terms(step)
+            if step + 1 < chunks:
+                reduce_angles(step + 1)
+            for inner in range(2):
+                renew(step, inner)
+        recall(0, 0, PN)
+        w2_mv.append(quantise_half("w2b", w2_raw[1], on_scalar, (fresh_staging(), fresh_staging())))
+        reduce_angles(4)
+        w3_mv.append(quantise_half("w3b", w3_raw[1], on_scalar, (fresh_staging(), fresh_staging())))
+        reduce_angles(5)
+        recall(1, 0, PN)
+        for step in (4, 5, 6):
+            for n in range(chunks + STAGE1_STEPS[step][1] // CHUNK, chunks + STAGE1_STEPS[step][2] // CHUNK):
+                make_terms(n)
+                if n + 2 < 2 * chunks:
+                    reduce_angles(n + 2)
+            for inner in range(2):
+                renew(step, inner)
+
+        w4_codes, w4_sc = mx_tiles("w4", H)
+        for part in range(2):
+            cols = slice(part * HALF, (part + 1) * HALF)
+            quantise_weight(w4_raw[part], w4_codes[:, cols], w4_sc[:, cols], nc.scalar.copy, fresh_staging())
+        for c in range(chunks):
+            round_x(banks[c % 2], 0, c)
 
         for lo, hi in ((0, CHUNK), (CHUNK, PN)):
             for t in range(2, TILES):
                 recall(t, lo, hi)
 
-        x_codes = work.tile([P, PN], U32, name="x_codes", tag="tab", bufs=2, align_bytes=64)
+        x_codes = work.tile([P, PN], U32, name="x_codes", tag="tab1", align_bytes=64)
         x_sc = keep.tile([P, PN], U8, name="x_sc", align_bytes=64)
 
-        def quantise_x(lo):
-            words = psum.tile([P, per_chunk, 2, P], F32, name="words", tag="tr", bufs=3)
-            round_x(1, lo // CHUNK)
+        def quantise_x(c, turned, words):
+            round_x(turned, 1, c)
             for b in range(per_chunk):
-                pairs = rounded[:, lo // P + b, :].bitcast(F32)
+                pairs = rounded[:, c * per_chunk + b, :].bitcast(F32)
                 for u in range(2):
-                    nc.tensor.transpose(words[:, b, u, :], pairs[:, u * P : (u + 1) * P], ident[:])
-            grouped = work.tile([P, CHUNK, PACK], BF16, name="grouped", tag="grouped", bufs=4, align_bytes=64)
+                    first = b * HALF + u * P
+                    nc.tensor.transpose(words[:, first : first + P], pairs[:, u * P : (u + 1) * P], ident[:])
+            grouped = fresh_staging()
             nc.scalar.copy(
-                grouped[:].rearrange("p j i -> p (j i)").bitcast(F32).rearrange("p (b j u) -> p b j u", b=per_chunk, u=2),
-                words[:].rearrange("p b u j -> p b j u"),
+                grouped.bitcast(F32).rearrange("p (b j u) -> p b j u", b=per_chunk, u=2),
+                words[:].rearrange("p (b u j) -> p b j u", b=per_chunk, u=2),
             )
-            cols = slice(lo, lo + CHUNK)
-            nc.vector.quantize_mx(
-                x_codes[:, cols].bitcast(FP8X4), x_sc[:, cols], grouped[:].rearrange("p j i -> p (j i)")
-            )
+            cols = slice(c * CHUNK, (c + 1) * CHUNK)
+            nc.vector.quantize_mx(x_codes[:, cols].bitcast(FP8X4), x_sc[:, cols], grouped)
 
-        def mix(t, lo, hi):
+        def mix(t, lo, hi, bank, y):
             rows = slice(t * P, (t + 1) * P)
-            mixed = psum.tile([P, hi - lo], F32, name="mixed", tag="mm", bufs=3)
             nc.tensor.matmul_mx(
-                mixed[:], lhsT=w4_codes[:, rows].bitcast(FP8X4), lhsT_scale=w4_sc[:, rows],
+                bank[:, : hi - lo], lhsT=w4_codes[:, rows].bitcast(FP8X4), lhsT_scale=w4_sc[:, rows],
                 rhs=x_codes[:, lo:hi].bitcast(FP8X4), rhs_scale=x_sc[:, lo:hi], start=True, stop=True,
             )
-            y = bounded[(lo // CHUNK % 2) * TILES + t][:, : hi - lo]
-            nc.scalar.copy(y, mixed[:])
-            if t >= 2:
-                weigh_x(t, lo, hi)
-            nc.gpsimd.tensor_tensor(y, y, aim_sb[t][:, lo:hi], ALU.mult)
-            return y
+            nc.vector.tensor_tensor(y, bank[:, : hi - lo], x[t][:, lo:hi], ALU.mult)
 
         def place(t, lo, hi, y):
-            nc.vector.tensor_copy(ration[t][:].indirect(entries(idx4, lo, hi)), y)
+            nc.vector.tensor_tensor(ration[t][:].indirect(entries(idx4, lo, hi)), y, wgo_sb[:, lo:hi], ALU.mult)
             if hi == PN:
                 nc.sync.dma_start(out[t * P : (t + 1) * P, :], ration[t][:])
 
-        for lo, hi in STAGE2_CHUNKS:
-            for part in range(lo, hi, CHUNK):
-                quantise_x(part)
-            ys = []
-            for t in range(TILES + 1):
-                if t > 0:
-                    ys_t = t - 1
-                if t < TILES:
-                    ys.append(mix(t, lo, hi))
-                if t > 0:
-                    place(ys_t, lo, hi, ys[ys_t])
+        def features(part, mixed_banks):
+            lo, hi = STAGE2_CHUNKS[part]
+            ys = [bounded[part % 2 * TILES + t][:, : hi - lo] for t in range(TILES)]
+            mix(0, lo, hi, banks[mixed_banks[0]], ys[0])
+            for t in range(TILES):
+                if t + 1 < TILES:
+                    mix(t + 1, lo, hi, banks[mixed_banks[t + 1]], ys[t + 1])
+                place(t, lo, hi, ys[t])
+
+        quantise_x(0, banks[0], banks[1])
+        features(0, (2, 3, 4, 5))
+        for c, turned, words in ((1, 2, 6), (2, 3, 7), (3, 4, 1)):
+            quantise_x(c, banks[turned], banks[words])
+        features(1, (0, 5, 2, 3))
+        features(2, (4, 6, 7, 1))

@@ -4,8 +4,8 @@ from contextlib import ExitStack
 import concourse.mybir as mybir
 from concourse.masks import make_identity
 
-K, T, S, H, T2, PN = 1024, 4096, 1024, 512, 2048, 1024
-FLOPS = 2 * (3 * K * H * S + H * H * PN)
+K, T, S, H, T2, RECALLED = 1024, 4096, 1024, 512, 2048, 1024
+FLOPS = 2 * (3 * K * H * S + H * H * RECALLED)
 
 F32 = mybir.dt.float32
 BF16 = mybir.dt.bfloat16
@@ -22,13 +22,17 @@ P = 128
 PACK = 4
 K_PASS = P * PACK
 PASSES = K // K_PASS
+QUADRANTS = 4
 TILES = H // P
-CHUNK = 256
-STAGE2_CHUNKS = ((0, 256), (256, 512), (512, 1024))
 HALF = H // 2
-RING = 4
 BANK = 512
-STAGE1_STEPS = ((0, 0, 256), (0, 256, 512), (0, 512, 768), (0, 768, 1024), (1, 0, 256), (1, 256, 512), (1, 512, 1024))
+CHUNK = 256
+BLOCKS = CHUNK // P
+CHUNKS = S // CHUNK
+RING = 4
+STEPS = ((0, 0, 256), (0, 256, 512), (0, 512, 768), (0, 768, 1024), (1, 0, 256), (1, 256, 512), (1, 512, 1024))
+PARTS = ((0, 256), (256, 512), (512, 1024))
+TWO_PI = 2.0 * math.pi
 
 
 def tile_list_falcon_ration_features_kernel(
@@ -43,15 +47,14 @@ def tile_list_falcon_ration_features_kernel(
 
         idx1 = lists.tile([P, S // 16], U16, name="idx1")
         idx2 = lists.tile([P, S // 16], U16, name="idx2")
-        idx3 = lists.tile([P, PN // 16], U16, name="idx3")
-        idx4 = lists.tile([P, PN // 16], U16, name="idx4")
+        idx3 = lists.tile([P, RECALLED // 16], U16, name="idx3")
+        idx4 = lists.tile([P, RECALLED // 16], U16, name="idx4")
 
         def entries(idx, lo, hi):
             return idx[:, lo // 16 : hi // 16]
 
-        tab_sc = [work.tile([P, T], U8, name=f"tab_sc{a}", tag="scales", bufs=2, align_bytes=64) for a in range(PASSES)]
-        for a in range(PASSES):
-            nc.vector.memset(tab_sc[a][:].bitcast(I32), 0)
+        tab_sc = work.tile([P, T], U8, name="tab_sc", tag="scales", bufs=2, align_bytes=64)
+        nc.vector.memset(tab_sc[:].bitcast(I32), 0)
         zero = keep.tile([P, 1], F32, name="zero")
         nc.vector.memset(zero[:], 0.0)
         zero_bias = keep.tile([P, 1], F32, name="zero_bias")
@@ -59,6 +62,8 @@ def tile_list_falcon_ration_features_kernel(
 
         w1_sc = keep.tile([P, PASSES, H], U8, name="w1_sc", align_bytes=64)
         nc.gpsimd.memset(w1_sc[:].rearrange("p a c -> p (a c)").bitcast(I32), 0)
+        v_sc_moved = keep.tile([P, S], U8, name="v_sc_moved", align_bytes=64)
+        nc.gpsimd.memset(v_sc_moved[:].bitcast(I32), 0)
         ident = keep.tile([P, P], F32, name="ident")
         make_identity(nc, ident[:])
 
@@ -69,8 +74,8 @@ def tile_list_falcon_ration_features_kernel(
         def load_table_pass(a):
             nc.sync.dma_start(tab[a][:], tab_words[a].rearrange("p t i -> p (t i)").bitcast(I32))
 
-        def load_weight(w, a, half):
-            raw = work.tile([P, PACK, HALF], F32, name="raw", tag="raw", bufs=4)
+        def load_weight(w, a, half, buffer):
+            raw = work.tile([P, PACK, HALF], F32, name="raw", tag=f"raw{buffer}")
             rows = w[a * K_PASS : (a + 1) * K_PASS, half * HALF : (half + 1) * HALF]
             nc.sync.dma_start(raw[:], rows.rearrange("(p i) c -> p i c", i=PACK))
             return raw
@@ -80,45 +85,46 @@ def tile_list_falcon_ration_features_kernel(
             nc.sync.dma_start(rows[:], src[t * P : (t + 1) * P, :])
             return rows
 
-        def load_table_scales(a):
-            for q in range(4):
-                nc.sync.dma_start(
-                    tab_sc[a][32 * q : 32 * q + 4, :].bitcast(I32), tab_scales[a, 4 * q : 4 * q + 4, :].bitcast(I32)
-                )
-
         load_table_pass(0)
-        load_table_scales(0)
-        w2_raw = [[load_weight(w2, a, 0) for a in range(PASSES)]]
-        load_table_scales(1)
+        for q in range(QUADRANTS):
+            nc.sync.dma_start(
+                tab_sc[32 * q : 32 * q + 8, :].bitcast(I32), tab_scales[:, 4 * q : 4 * q + 4, :].bitcast(I32)
+            )
         load_table_pass(1)
         w1_codes = keep.tile([P, PASSES, 2 * H], U8, name="w1_codes", align_bytes=64)
         nc.sync.dma_start(w1_codes[:].bitcast(I32), w1_words.rearrange("a p c -> p a c").bitcast(I32))
-        w3_raw = [[load_weight(w3, a, 0) for a in range(PASSES)]]
+        w2_raw = [[load_weight(w2, 0, 0, 0)]]
 
         v = [keep.tile([P, S], U32, name=f"v{a}", align_bytes=64) for a in range(PASSES)]
         nc.vector.tensor_copy(v[0][:], tab[0][:].bitcast(U32).indirect(idx1[:]))
-        v_sc = [keep.tile([P, S], U8, name=f"v_sc{a}", align_bytes=64) for a in range(PASSES)]
-        for a in range(PASSES):
-            nc.vector.tensor_copy(v_sc[a][:], tab_sc[a][:].indirect(idx1[:]))
+        v_sc = keep.tile([P, S], U8, name="v_sc", align_bytes=64)
+        nc.vector.tensor_copy(v_sc[:], tab_sc[:].indirect(idx1[:]))
+        nc.vector.tensor_copy(v[1][:], tab[1][:].bitcast(U32).indirect(idx1[:]))
+        for q in range(QUADRANTS):
+            nc.sync.dma_start(
+                v_sc_moved[32 * q : 32 * q + 4, :].bitcast(I32), v_sc[32 * q + 4 : 32 * q + 8, :].bitcast(I32)
+            )
 
+        w2_raw[0].append(load_weight(w2, 1, 0, 1))
+        w3_raw = [[load_weight(w3, a, 0, 2 + a) for a in range(PASSES)]]
         nc.sync.dma_start(idx2[:], offs2)
         wgs_sb = load_rows("wgs_sb", wgs, 0)
-        page = [load_rows("states", page0, t) for t in range(2)]
-        w2_raw.append([load_weight(w2, a, 1) for a in range(PASSES)])
-        w3_raw.append([load_weight(w3, a, 1) for a in range(PASSES)])
+        states = [load_rows("states", page0, t) for t in range(2)]
+        w2_raw.append([load_weight(w2, a, 1, a) for a in range(PASSES)])
+        w3_raw.append([load_weight(w3, a, 1, 2 + a) for a in range(PASSES)])
         nc.sync.dma_start(idx3[:], offs3)
-        aim_sb = [load_rows("aims", aim, t) for t in range(2)]
-        page.extend([load_rows("states", page0, t) for t in range(2, TILES)])
+        aims = [load_rows("aims", aim, t) for t in range(2)]
+        states.extend([load_rows("states", page0, t) for t in range(2, TILES)])
         for t in range(2, TILES):
-            late_aim = work.tile([P, PN], F32, name="late_aim", tag="scales", bufs=2, align_bytes=64)
+            late_aim = work.tile([P, RECALLED], F32, name="late_aim", tag="scales", bufs=2, align_bytes=64)
             nc.sync.dma_start(late_aim[:], aim[t * P : (t + 1) * P, :])
-            aim_sb.append(late_aim)
-        w4_raw = [load_weight(w4, 0, half) for half in range(2)]
+            aims.append(late_aim)
+        w4_raw = [load_weight(w4, 0, half, half) for half in range(2)]
         wgo_sb = load_rows("wgo_sb", wgo, 0)
         nc.sync.dma_start(idx4[:], offs4)
         ration = [load_rows("ration", page1, t) for t in range(TILES)]
 
-        for q in range(4):
+        for q in range(QUADRANTS):
             nc.gpsimd.dma_start(
                 w1_sc[32 * q : 32 * q + 4, :, :].bitcast(I32),
                 w1_scales[:, 4 * q : 4 * q + 4, :].rearrange("a r c -> r a c").bitcast(I32),
@@ -129,206 +135,201 @@ def tile_list_falcon_ration_features_kernel(
         neg_gain = keep.tile([P, TILES], F32, name="neg_gain")
         nc.gpsimd.tensor_scalar(neg_gain[:], gain_sb[:], -1.0, 0.0, ALU.mult, ALU.add)
 
+        def staging():
+            grouped = work.tile([P, HALF * PACK], BF16, name="grouped", tag="grouped", bufs=4, align_bytes=64)
+            return grouped[:]
+
         def quantise_weight(raw, codes, scales, copy, grouped):
             copy(grouped.rearrange("p (c e i) -> p c i e", e=4, i=PACK), raw[:].rearrange("p i (c e) -> p c i e", e=4))
             nc.vector.quantize_mx(codes.bitcast(FP8X4), scales, grouped)
 
-        def fresh_staging():
-            grouped = work.tile([P, HALF * PACK], BF16, name="grouped", tag="grouped", bufs=4, align_bytes=64)
-            return grouped[:]
-
         waves = [keep.tile([P, H], F32, name=f"wave{i}", align_bytes=64) for i in range(RING)]
         bares = [keep.tile([P, H], F32, name=f"bare{i}", align_bytes=64) for i in range(RING)]
-
 
         def mx_tiles(name, width):
             codes = keep.tile([P, width], U32, name=name + "_codes", align_bytes=64)
             scales = keep.tile([P, width], U8, name=name + "_sc", align_bytes=64)
             return codes, scales
 
-        def quantise_half(name, raws, copies, staging):
+        def quantise_half(name, raws, copies):
+            staged = [staging() for a in range(PASSES)]
             made = []
             for a in range(PASSES):
                 codes, scales = mx_tiles(f"{name}_{a}", HALF)
-                quantise_weight(raws[a], codes[:], scales[:], copies[a], staging[a])
+                quantise_weight(raws[a], codes[:], scales[:], copies[a], staged[a])
                 made.append((codes[:].bitcast(FP8X4), scales[:]))
             return made
 
-        def first_product(sums, jb, moving):
-            cols = slice(jb * P, (jb + 1) * P)
+        v_sc_shared = [v_sc[4 * a : P, :] for a in range(PASSES)]
+        v_sc_from_zero = [v_sc[:], v_sc_moved[:]]
+
+        def first_product(sums, block, weight, v_scales):
+            cols = slice(block * P, (block + 1) * P)
             for a in range(PASSES):
-                codes, scales = moving[a]
+                codes, scales = weight[a]
                 nc.tensor.matmul_mx(
-                    sums, lhsT=v[a][:, cols].bitcast(FP8X4), lhsT_scale=v_sc[a][:, cols],
+                    sums, lhsT=v[a][:, cols].bitcast(FP8X4), lhsT_scale=v_scales[a][:, cols],
                     rhs=codes, rhs_scale=scales, start=(a == 0), stop=(a == PASSES - 1),
                 )
 
-        per_chunk = CHUNK // P
-        chunks = S // CHUNK
-
-        def half_product(bank, c, moving):
-            for b in range(per_chunk):
-                first_product(bank[:, b * HALF : (b + 1) * HALF], c * per_chunk + b, moving)
+        def unit_product(bank, chunk, weight):
+            for b in range(BLOCKS):
+                first_product(bank[:, b * HALF : (b + 1) * HALF], chunk * BLOCKS + b, weight, v_sc_shared)
 
         on_scalar = (nc.scalar.copy, nc.scalar.copy)
-        w1_mv = [(w1_codes[:, a, :].bitcast(FP4X4), w1_sc[:, a, :]) for a in range(PASSES)]
-        w2_mv = [quantise_half("w2a", w2_raw[0], on_scalar, (fresh_staging(), fresh_staging()))]
-        for lo in range(0, S, S // 2):
-            nc.vector.tensor_copy(
-                v[1][:, lo : lo + S // 2], tab[1][:].bitcast(U32).indirect(entries(idx1, lo, lo + S // 2))
-            )
-        w3_mv = [quantise_half("w3a", w3_raw[0], (nc.vector.tensor_copy, nc.scalar.copy), (fresh_staging(), fresh_staging()))]
+        w1_mx = [(w1_codes[:, a, :].bitcast(FP4X4), w1_sc[:, a, :]) for a in range(PASSES)]
+        w2_mx = [quantise_half("w2a", w2_raw[0], (nc.scalar.copy, nc.vector.tensor_copy))]
+        w3_mx = [quantise_half("w3a", w3_raw[0], (nc.vector.tensor_copy, nc.vector.tensor_copy))]
 
-        x = [keep.tile([P, PN], F32, name=f"x{t}") for t in range(TILES)]
+        x = [keep.tile([P, RECALLED], F32, name=f"x{t}") for t in range(TILES)]
         turns_ring = [keep.tile([P, H], I32, name=f"turns{i}") for i in range(2)]
 
-        def angle_of(n):
-            return x[n // 2][:, n % 2 * H : (n % 2 + 1) * H]
+        def angle_of(unit):
+            return x[unit // 2][:, unit % 2 * H : (unit % 2 + 1) * H]
 
-        def reduce_angles(n):
-            half, c = divmod(n, chunks)
-            bank = banks[n % 2]
-            half_product(bank, c, w2_mv[half])
-            if n // 2 == 2:
-                turns = x[1][:, n % 2 * H : (n % 2 + 1) * H].bitcast(I32)
+        def reduce_angles(unit):
+            half, chunk = divmod(unit, CHUNKS)
+            bank = banks[unit % 2]
+            unit_product(bank, chunk, w2_mx[half])
+            if half == 1 and chunk < 2:
+                turns = x[chunk][:, :H].bitcast(I32)
             else:
-                turns = turns_ring[n % 2][:]
-            if n >= 6:
-                nc.scalar.activation(angle_of(n), bank[:], ACT.Abs, bias=zero_bias[:])
-                nc.scalar.activation(turns.bitcast(U32), angle_of(n), ACT.Copy, bias=0.25, scale=1.0 / (2.0 * math.pi))
-                nc.vector.scalar_tensor_tensor(angle_of(n), turns, -2.0 * math.pi, angle_of(n), ALU.mult, ALU.add)
-            else:
-                nc.vector.tensor_scalar(turns, bank[:], 1.0 / (2.0 * math.pi), None, ALU.mult)
-                nc.vector.scalar_tensor_tensor(angle_of(n), turns, -2.0 * math.pi, bank[:], ALU.mult, ALU.add)
-
-        bounded = [keep.tile([P, H], F32, name=f"bounded{jb}") for jb in range(S // P)]
-
-        def bound(jb):
-            bank = banks[2 + jb % 2]
-            first_product(bank[:], jb, w1_mv)
-            nc.scalar.activation(bounded[jb][:], bank[:], ACT.Tanh, bias=zero_bias[:], scale=-1.0)
-
-        def make_terms(n):
-            half, c = divmod(n, chunks)
+                turns = turns_ring[unit % 2][:]
             if half == 0:
-                for b in range(per_chunk):
-                    bound(c * per_chunk + b)
-            wave = waves[n % RING][:]
-            nc.scalar.activation(wave, angle_of(n), ACT.Sin, bias=zero_bias[:], scale=0.5)
+                nc.vector.tensor_scalar(turns, bank[:], 1.0 / TWO_PI, None, ALU.mult)
+                nc.vector.scalar_tensor_tensor(angle_of(unit), turns, -TWO_PI, bank[:], ALU.mult, ALU.add)
+            else:
+                nc.scalar.activation(angle_of(unit), bank[:], ACT.Abs, bias=zero_bias[:])
+                nc.scalar.activation(turns.bitcast(U32), angle_of(unit), ACT.Copy, bias=0.25, scale=1.0 / TWO_PI)
+                nc.vector.scalar_tensor_tensor(angle_of(unit), turns, -TWO_PI, angle_of(unit), ALU.mult, ALU.add)
+
+        bounded = [keep.tile([P, H], F32, name=f"bounded{block}") for block in range(S // P)]
+
+        def bound(block):
+            bank = banks[2 + block % 2]
+            first_product(bank[:], block, w1_mx, v_sc_from_zero)
+            nc.scalar.activation(bounded[block][:], bank[:], ACT.Tanh, bias=zero_bias[:], scale=-1.0)
+
+        def make_terms(unit):
+            half, chunk = divmod(unit, CHUNKS)
+            if half == 0:
+                for b in range(BLOCKS):
+                    bound(chunk * BLOCKS + b)
+            wave = waves[unit % RING][:]
+            nc.scalar.activation(wave, angle_of(unit), ACT.Sin, bias=zero_bias[:], scale=0.5)
             nc.scalar.activation(wave, wave, ACT.Square, bias=zero_bias[:], scale=math.sqrt(2.0))
-            bank = banks[4] if half == 0 else banks[3 + n % 2]
-            half_product(bank, c, w3_mv[half])
-            nc.scalar.activation(bares[n % RING][:], bank[:], ACT.Copy, bias=-1.0, scale=-1.0)
+            bank = banks[4] if half == 0 else banks[3 + unit % 2]
+            unit_product(bank, chunk, w3_mx[half])
+            nc.scalar.activation(bares[unit % RING][:], bank[:], ACT.Copy, bias=-1.0, scale=-1.0)
 
         h_ring = [keep.tile([P, 2 * CHUNK], F32, name=f"h{i}") for i in range(RING)]
 
         def renew(step, inner):
-            half, lo, hi = STAGE1_STEPS[step]
+            half, lo, hi = STEPS[step]
             t = 2 * half + inner
             total = banks[5 + (2 * step + inner) % 3]
-            for jb in range(lo // P, hi // P):
-                slot = (half * chunks + jb // per_chunk) % RING
-                first = jb % per_chunk * HALF + inner * P
+            for block in range(lo // P, hi // P):
+                slot = (half * CHUNKS + block // BLOCKS) % RING
+                first = block % BLOCKS * HALF + inner * P
                 terms = (
-                    bounded[jb][:, t * P : (t + 1) * P],
-                    waves[slot][:, first : first + P],
                     bares[slot][:, first : first + P],
+                    waves[slot][:, first : first + P],
+                    bounded[block][:, t * P : (t + 1) * P],
                 )
                 for m, term in enumerate(terms):
                     nc.tensor.matmul(
-                        total[:, jb * P - lo : (jb + 1) * P - lo], lhsT=term, rhs=ident[:],
-                        is_transpose=True, start=(m == 0), stop=(m == 2),
+                        total[:, block * P - lo : (block + 1) * P - lo], lhsT=term, rhs=ident[:],
+                        is_transpose=True, start=(m == 0), stop=(m == len(terms) - 1),
                     )
             h = h_ring[(2 * step + inner) % RING][:, : hi - lo]
             nc.scalar.activation(h, total[:, : hi - lo], ACT.Copy, scale=neg_gain[:, t : t + 1])
-            nc.vector.tensor_tensor(page[t][:].indirect(entries(idx2, lo, hi)), h, wgs_sb[:, lo:hi], ALU.mult)
+            nc.vector.tensor_tensor(states[t][:].indirect(entries(idx2, lo, hi)), h, wgs_sb[:, lo:hi], ALU.mult)
 
         def recall(t, lo, hi):
             nc.vector.tensor_tensor(
-                x[t][:, lo:hi], page[t][:].indirect(entries(idx3, lo, hi)), aim_sb[t][:, lo:hi], ALU.subtract
+                x[t][:, lo:hi], states[t][:].indirect(entries(idx3, lo, hi)), aims[t][:, lo:hi], ALU.subtract
             )
 
-        rounded = work.tile([P, PN // P, H], BF16, name="rounded", tag="tab0", align_bytes=64)
+        rounded = work.tile([P, RECALLED // P, H], BF16, name="rounded", tag="tab0", align_bytes=64)
 
-        def round_x(turned, half, c):
-            for b in range(per_chunk):
-                jb = c * per_chunk + b
+        def round_x(turned, half, chunk):
+            for b in range(BLOCKS):
+                block = chunk * BLOCKS + b
                 for inner in range(2):
                     first = b * HALF + inner * P
                     nc.tensor.transpose(
-                        turned[:, first : first + P], x[2 * half + inner][:, jb * P : (jb + 1) * P], ident[:]
+                        turned[:, first : first + P], x[2 * half + inner][:, block * P : (block + 1) * P], ident[:]
                     )
-            blocks = rounded[:, c * per_chunk : (c + 1) * per_chunk, :]
+            rows = rounded[:, chunk * BLOCKS : (chunk + 1) * BLOCKS, :]
             nc.scalar.copy(
-                blocks.rearrange("j b (u h p e) -> j b u h p e", u=2, h=2, e=2)[:, :, :, half, :, :],
-                turned[:].rearrange("j (b p u e) -> j b u p e", b=per_chunk, u=2, e=2),
+                rows.rearrange("j b (u g p e) -> j b u g p e", u=2, g=2, e=2)[:, :, :, half, :, :],
+                turned[:].rearrange("j (b p u e) -> j b u p e", b=BLOCKS, u=2, e=2),
             )
 
         reduce_angles(0)
-        for step in range(chunks):
+        for step in range(CHUNKS):
             make_terms(step)
-            if step + 1 < chunks:
+            if step + 1 < CHUNKS:
                 reduce_angles(step + 1)
             for inner in range(2):
                 renew(step, inner)
-        recall(0, 0, PN)
-        w2_mv.append(quantise_half("w2b", w2_raw[1], on_scalar, (fresh_staging(), fresh_staging())))
-        reduce_angles(4)
-        w3_mv.append(quantise_half("w3b", w3_raw[1], on_scalar, (fresh_staging(), fresh_staging())))
-        reduce_angles(5)
-        recall(1, 0, PN)
-        for step in (4, 5, 6):
-            for n in range(chunks + STAGE1_STEPS[step][1] // CHUNK, chunks + STAGE1_STEPS[step][2] // CHUNK):
-                make_terms(n)
-                if n + 2 < 2 * chunks:
-                    reduce_angles(n + 2)
+        w2_mx.append(quantise_half("w2b", w2_raw[1], on_scalar))
+        w3_mx.append(quantise_half("w3b", w3_raw[1], on_scalar))
+        for t in range(2):
+            reduce_angles(CHUNKS + t)
+            recall(t, 0, RECALLED)
+        for step in range(CHUNKS, len(STEPS)):
+            for unit in range(CHUNKS + STEPS[step][1] // CHUNK, CHUNKS + STEPS[step][2] // CHUNK):
+                make_terms(unit)
+                if unit + 2 < 2 * CHUNKS:
+                    reduce_angles(unit + 2)
             for inner in range(2):
                 renew(step, inner)
 
         w4_codes, w4_sc = mx_tiles("w4", H)
-        for part in range(2):
-            cols = slice(part * HALF, (part + 1) * HALF)
-            quantise_weight(w4_raw[part], w4_codes[:, cols], w4_sc[:, cols], nc.scalar.copy, fresh_staging())
-        for c in range(chunks):
-            round_x(banks[c % 2], 0, c)
+        for half in range(2):
+            cols = slice(half * HALF, (half + 1) * HALF)
+            quantise_weight(w4_raw[half], w4_codes[:, cols], w4_sc[:, cols], nc.scalar.copy, staging())
+        for chunk in range(RECALLED // CHUNK):
+            round_x(banks[chunk % 2], 0, chunk)
 
-        for lo, hi in ((0, CHUNK), (CHUNK, PN)):
+        for lo, hi in ((0, CHUNK), (CHUNK, RECALLED)):
             for t in range(2, TILES):
                 recall(t, lo, hi)
 
-        x_codes = work.tile([P, PN], U32, name="x_codes", tag="tab1", align_bytes=64)
-        x_sc = keep.tile([P, PN], U8, name="x_sc", align_bytes=64)
+        x_codes = work.tile([P, RECALLED], U32, name="x_codes", tag="tab1", align_bytes=64)
+        x_sc = keep.tile([P, RECALLED], U8, name="x_sc", align_bytes=64)
 
-        def quantise_x(c, turned, words):
-            round_x(turned, 1, c)
-            for b in range(per_chunk):
-                pairs = rounded[:, c * per_chunk + b, :].bitcast(F32)
+        def quantise_x(chunk, turned, words):
+            round_x(turned, 1, chunk)
+            for b in range(BLOCKS):
+                pairs = rounded[:, chunk * BLOCKS + b, :].bitcast(F32)
                 for u in range(2):
                     first = b * HALF + u * P
                     nc.tensor.transpose(words[:, first : first + P], pairs[:, u * P : (u + 1) * P], ident[:])
-            grouped = fresh_staging()
+            grouped = staging()
             nc.scalar.copy(
-                grouped.bitcast(F32).rearrange("p (b j u) -> p b j u", b=per_chunk, u=2),
-                words[:].rearrange("p (b u j) -> p b j u", b=per_chunk, u=2),
+                grouped.bitcast(F32).rearrange("p (b j u) -> p b j u", b=BLOCKS, u=2),
+                words[:].rearrange("p (b u j) -> p b j u", b=BLOCKS, u=2),
             )
-            cols = slice(c * CHUNK, (c + 1) * CHUNK)
+            cols = slice(chunk * CHUNK, (chunk + 1) * CHUNK)
             nc.vector.quantize_mx(x_codes[:, cols].bitcast(FP8X4), x_sc[:, cols], grouped)
 
         def mix(t, lo, hi, bank, y):
-            rows = slice(t * P, (t + 1) * P)
+            channels = slice(t * P, (t + 1) * P)
             nc.tensor.matmul_mx(
-                bank[:, : hi - lo], lhsT=w4_codes[:, rows].bitcast(FP8X4), lhsT_scale=w4_sc[:, rows],
+                bank[:, : hi - lo], lhsT=w4_codes[:, channels].bitcast(FP8X4), lhsT_scale=w4_sc[:, channels],
                 rhs=x_codes[:, lo:hi].bitcast(FP8X4), rhs_scale=x_sc[:, lo:hi], start=True, stop=True,
             )
             nc.vector.tensor_tensor(y, bank[:, : hi - lo], x[t][:, lo:hi], ALU.mult)
 
         def place(t, lo, hi, y):
             nc.vector.tensor_tensor(ration[t][:].indirect(entries(idx4, lo, hi)), y, wgo_sb[:, lo:hi], ALU.mult)
-            if hi == PN:
+            if hi == RECALLED:
                 nc.sync.dma_start(out[t * P : (t + 1) * P, :], ration[t][:])
 
         def features(part, mixed_banks):
-            lo, hi = STAGE2_CHUNKS[part]
+            lo, hi = PARTS[part]
             ys = [bounded[part % 2 * TILES + t][:, : hi - lo] for t in range(TILES)]
             mix(0, lo, hi, banks[mixed_banks[0]], ys[0])
             for t in range(TILES):
@@ -338,7 +339,7 @@ def tile_list_falcon_ration_features_kernel(
 
         quantise_x(0, banks[0], banks[1])
         features(0, (2, 3, 4, 5))
-        for c, turned, words in ((1, 2, 6), (2, 3, 7), (3, 4, 1)):
-            quantise_x(c, banks[turned], banks[words])
+        for chunk, turned, words in ((1, 2, 6), (2, 3, 7), (3, 4, 1)):
+            quantise_x(chunk, banks[turned], banks[words])
         features(1, (0, 5, 2, 3))
         features(2, (4, 6, 7, 1))

import math
from contextlib import ExitStack

import concourse.mybir as mybir
from concourse.masks import make_identity

K, T, S, H, T2, RECALLED = 1024, 4096, 1024, 512, 2048, 1024
FLOPS = 2 * (3 * K * H * S + H * H * RECALLED)

F32 = mybir.dt.float32
BF16 = mybir.dt.bfloat16
I32 = mybir.dt.int32
U32 = mybir.dt.uint32
U16 = mybir.dt.uint16
U8 = mybir.dt.uint8
FP8X4 = mybir.dt.float8_e4m3fn_x4
FP4X4 = mybir.dt.float4_e2m1fn_x4
ALU = mybir.AluOpType
ACT = mybir.ActivationFunctionType

P = 128
PACK = 4
K_PASS = P * PACK
PASSES = K // K_PASS
QUADRANTS = 4
TILES = H // P
HALF = H // 2
BANK = 512
CHUNK = 256
BLOCKS = CHUNK // P
CHUNKS = S // CHUNK
RING = 4
STEPS = ((0, 0, 256), (0, 256, 512), (0, 512, 768), (0, 768, 1024), (1, 0, 256), (1, 256, 512), (1, 512, 1024))
PARTS = ((0, 256), (256, 512), (512, 1024))
TWO_PI = 2.0 * math.pi


def tile_list_falcon_ration_features_kernel(
    tc, tab_words, tab_scales, offs, offs2, offs3, offs4, w1_words, w1_scales, w2, w3, gain, wgs, page0, aim, w4, wgo, page1, out
):
    nc = tc.nc
    with ExitStack() as ctx:
        lists = ctx.enter_context(tc.tile_pool(name="lists", bufs=1))
        keep = ctx.enter_context(tc.tile_pool(name="keep", bufs=1))
        work = ctx.enter_context(tc.tile_pool(name="work", bufs=1))
        psum = ctx.enter_context(tc.psum_pool(name="psum", bufs=1))

        idx1 = lists.tile([P, S // 16], U16, name="idx1")
        idx2 = lists.tile([P, S // 16], U16, name="idx2")
        idx3 = lists.tile([P, RECALLED // 16], U16, name="idx3")
        idx4 = lists.tile([P, RECALLED // 16], U16, name="idx4")

        def entries(idx, lo, hi):
            return idx[:, lo // 16 : hi // 16]

        tab_sc = work.tile([P, T], U8, name="tab_sc", tag="scales", bufs=2, align_bytes=64)
        nc.vector.memset(tab_sc[:].bitcast(I32), 0)
        zero = keep.tile([P, 1], F32, name="zero")
        nc.vector.memset(zero[:], 0.0)
        zero_bias = keep.tile([P, 1], F32, name="zero_bias")
        nc.scalar.activation(zero_bias[:], zero[:], ACT.Silu)

        w1_sc = keep.tile([P, PASSES, H], U8, name="w1_sc", align_bytes=64)
        nc.gpsimd.memset(w1_sc[:].rearrange("p a c -> p (a c)").bitcast(I32), 0)
        v_sc_moved = keep.tile([P, S], U8, name="v_sc_moved", align_bytes=64)
        nc.gpsimd.memset(v_sc_moved[:].bitcast(I32), 0)
        ident = keep.tile([P, P], F32, name="ident")
        make_identity(nc, ident[:])

        nc.sync.dma_start(idx1[:], offs)
        tab = [work.tile([P, T], I32, name=f"tab{a}", tag=f"tab{a}", align_bytes=64) for a in range(PASSES)]
        banks = [psum.tile([P, BANK], F32, name=f"bank{i}") for i in range(8)]

        def load_table_pass(a):
            nc.sync.dma_start(tab[a][:], tab_words[a].rearrange("p t i -> p (t i)").bitcast(I32))

        def load_weight(w, a, half, buffer):
            raw = work.tile([P, PACK, HALF], F32, name="raw", tag=f"raw{buffer}")
            rows = w[a * K_PASS : (a + 1) * K_PASS, half * HALF : (half + 1) * HALF]
            nc.sync.dma_start(raw[:], rows.rearrange("(p i) c -> p i c", i=PACK))
            return raw

        def load_rows(name, src, t):
            rows = keep.tile([P, src.shape[1]], F32, name=f"{name}{t}")
            nc.sync.dma_start(rows[:], src[t * P : (t + 1) * P, :])
            return rows

        load_table_pass(0)
        for q in range(QUADRANTS):
            nc.sync.dma_start(
                tab_sc[32 * q : 32 * q + 8, :].bitcast(I32), tab_scales[:, 4 * q : 4 * q + 4, :].bitcast(I32)
            )
        load_table_pass(1)
        w1_codes = keep.tile([P, PASSES, 2 * H], U8, name="w1_codes", align_bytes=64)
        nc.sync.dma_start(w1_codes[:].bitcast(I32), w1_words.rearrange("a p c -> p a c").bitcast(I32))
        w2_raw = [[load_weight(w2, 0, 0, 0)]]

        v = [keep.tile([P, S], U32, name=f"v{a}", align_bytes=64) for a in range(PASSES)]
        nc.vector.tensor_copy(v[0][:], tab[0][:].bitcast(U32).indirect(idx1[:]))
        v_sc = keep.tile([P, S], U8, name="v_sc", align_bytes=64)
        nc.vector.tensor_copy(v_sc[:], tab_sc[:].indirect(idx1[:]))
        nc.vector.tensor_copy(v[1][:], tab[1][:].bitcast(U32).indirect(idx1[:]))
        for q in range(QUADRANTS):
            nc.sync.dma_start(
                v_sc_moved[32 * q : 32 * q + 4, :].bitcast(I32), v_sc[32 * q + 4 : 32 * q + 8, :].bitcast(I32)
            )

        w2_raw[0].append(load_weight(w2, 1, 0, 1))
        w3_raw = [[load_weight(w3, a, 0, 2 + a) for a in range(PASSES)]]
        nc.sync.dma_start(idx2[:], offs2)
        wgs_sb = load_rows("wgs_sb", wgs, 0)
        states = [load_rows("states", page0, t) for t in range(2)]
        w2_raw.append([load_weight(w2, a, 1, a) for a in range(PASSES)])
        w3_raw.append([load_weight(w3, a, 1, 2 + a) for a in range(PASSES)])
        nc.sync.dma_start(idx3[:], offs3)
        aims = [load_rows("aims", aim, t) for t in range(2)]
        states.extend([load_rows("states", page0, t) for t in range(2, TILES)])
        for t in range(2, TILES):
            late_aim = work.tile([P, RECALLED], F32, name="late_aim", tag="scales", bufs=2, align_bytes=64)
            nc.sync.dma_start(late_aim[:], aim[t * P : (t + 1) * P, :])
            aims.append(late_aim)
        w4_raw = [load_weight(w4, 0, half, half) for half in range(2)]
        wgo_sb = load_rows("wgo_sb", wgo, 0)
        nc.sync.dma_start(idx4[:], offs4)
        ration = [load_rows("ration", page1, t) for t in range(TILES)]

        for q in range(QUADRANTS):
            nc.gpsimd.dma_start(
                w1_sc[32 * q : 32 * q + 4, :, :].bitcast(I32),
                w1_scales[:, 4 * q : 4 * q + 4, :].rearrange("a r c -> r a c").bitcast(I32),
            )
        gain_sb = keep.tile([P, TILES], F32, name="gain_sb")
        with nc.allow_non_contiguous_dma(reason="one gain value for each partition and tile"):
            nc.gpsimd.dma_start(gain_sb[:], gain.rearrange("(t p) -> p t", p=P))
        neg_gain = keep.tile([P, TILES], F32, name="neg_gain")
        nc.gpsimd.tensor_scalar(neg_gain[:], gain_sb[:], -1.0, 0.0, ALU.mult, ALU.add)

        def staging():
            grouped = work.tile([P, HALF * PACK], BF16, name="grouped", tag="grouped", bufs=4, align_bytes=64)
            return grouped[:]

        def quantise_weight(raw, codes, scales, copy, grouped):
            copy(grouped.rearrange("p (c e i) -> p c i e", e=4, i=PACK), raw[:].rearrange("p i (c e) -> p c i e", e=4))
            nc.vector.quantize_mx(codes.bitcast(FP8X4), scales, grouped)

        waves = [keep.tile([P, H], F32, name=f"wave{i}", align_bytes=64) for i in range(RING)]
        bares = [keep.tile([P, H], F32, name=f"bare{i}", align_bytes=64) for i in range(RING)]

        def mx_tiles(name, width):
            codes = keep.tile([P, width], U32, name=name + "_codes", align_bytes=64)
            scales = keep.tile([P, width], U8, name=name + "_sc", align_bytes=64)
            return codes, scales

        def quantise_half(name, raws, copies):
            staged = [staging() for a in range(PASSES)]
            made = []
            for a in range(PASSES):
                codes, scales = mx_tiles(f"{name}_{a}", HALF)
                quantise_weight(raws[a], codes[:], scales[:], copies[a], staged[a])
                made.append((codes[:].bitcast(FP8X4), scales[:]))
            return made

        v_sc_shared = [v_sc[4 * a : P, :] for a in range(PASSES)]
        v_sc_from_zero = [v_sc[:], v_sc_moved[:]]

        def first_product(sums, block, weight, v_scales):
            cols = slice(block * P, (block + 1) * P)
            for a in range(PASSES):
                codes, scales = weight[a]
                nc.tensor.matmul_mx(
                    sums, lhsT=v[a][:, cols].bitcast(FP8X4), lhsT_scale=v_scales[a][:, cols],
                    rhs=codes, rhs_scale=scales, start=(a == 0), stop=(a == PASSES - 1),
                )

        def unit_product(bank, chunk, weight):
            for b in range(BLOCKS):
                first_product(bank[:, b * HALF : (b + 1) * HALF], chunk * BLOCKS + b, weight, v_sc_shared)

        on_scalar = (nc.scalar.copy, nc.scalar.copy)
        w1_mx = [(w1_codes[:, a, :].bitcast(FP4X4), w1_sc[:, a, :]) for a in range(PASSES)]
        w2_mx = [quantise_half("w2a", w2_raw[0], (nc.scalar.copy, nc.vector.tensor_copy))]
        w3_mx = [quantise_half("w3a", w3_raw[0], (nc.vector.tensor_copy, nc.vector.tensor_copy))]

        x = [keep.tile([P, RECALLED], F32, name=f"x{t}") for t in range(TILES)]
        turns_ring = [keep.tile([P, H], I32, name=f"turns{i}") for i in range(2)]

        def angle_of(unit):
            return x[unit // 2][:, unit % 2 * H : (unit % 2 + 1) * H]

        def reduce_angles(unit):
            half, chunk = divmod(unit, CHUNKS)
            bank = banks[unit % 2]
            unit_product(bank, chunk, w2_mx[half])
            if half == 1 and chunk < 2:
                turns = x[chunk][:, :H].bitcast(I32)
            else:
                turns = turns_ring[unit % 2][:]
            if half == 0:
                nc.vector.tensor_scalar(turns, bank[:], 1.0 / TWO_PI, None, ALU.mult)
                nc.vector.scalar_tensor_tensor(angle_of(unit), turns, -TWO_PI, bank[:], ALU.mult, ALU.add)
            else:
                nc.scalar.activation(angle_of(unit), bank[:], ACT.Abs, bias=zero_bias[:])
                nc.scalar.activation(turns.bitcast(U32), angle_of(unit), ACT.Copy, bias=0.25, scale=1.0 / TWO_PI)
                nc.vector.scalar_tensor_tensor(angle_of(unit), turns, -TWO_PI, angle_of(unit), ALU.mult, ALU.add)

        bounded = [keep.tile([P, H], F32, name=f"bounded{block}") for block in range(S // P)]

        def bound(block):
            bank = banks[2 + block % 2]
            first_product(bank[:], block, w1_mx, v_sc_from_zero)
            nc.scalar.activation(bounded[block][:], bank[:], ACT.Tanh, bias=zero_bias[:], scale=-1.0)

        def make_terms(unit):
            half, chunk = divmod(unit, CHUNKS)
            if half == 0:
                for b in range(BLOCKS):
                    bound(chunk * BLOCKS + b)
            wave = waves[unit % RING][:]
            nc.scalar.activation(wave, angle_of(unit), ACT.Sin, bias=zero_bias[:], scale=0.5)
            nc.scalar.activation(wave, wave, ACT.Square, bias=zero_bias[:], scale=math.sqrt(2.0))
            bank = banks[4] if half == 0 else banks[3 + unit % 2]
            unit_product(bank, chunk, w3_mx[half])
            nc.scalar.activation(bares[unit % RING][:], bank[:], ACT.Copy, bias=-1.0, scale=-1.0)

        h_ring = [keep.tile([P, 2 * CHUNK], F32, name=f"h{i}") for i in range(RING)]

        def renew(step, inner):
            half, lo, hi = STEPS[step]
            t = 2 * half + inner
            total = banks[5 + (2 * step + inner) % 3]
            for block in range(lo // P, hi // P):
                slot = (half * CHUNKS + block // BLOCKS) % RING
                first = block % BLOCKS * HALF + inner * P
                terms = (
                    bares[slot][:, first : first + P],
                    waves[slot][:, first : first + P],
                    bounded[block][:, t * P : (t + 1) * P],
                )
                for m, term in enumerate(terms):
                    nc.tensor.matmul(
                        total[:, block * P - lo : (block + 1) * P - lo], lhsT=term, rhs=ident[:],
                        is_transpose=True, start=(m == 0), stop=(m == len(terms) - 1),
                    )
            h = h_ring[(2 * step + inner) % RING][:, : hi - lo]
            nc.scalar.activation(h, total[:, : hi - lo], ACT.Copy, scale=neg_gain[:, t : t + 1])
            nc.vector.tensor_tensor(states[t][:].indirect(entries(idx2, lo, hi)), h, wgs_sb[:, lo:hi], ALU.mult)

        def recall(t, lo, hi):
            nc.vector.tensor_tensor(
                x[t][:, lo:hi], states[t][:].indirect(entries(idx3, lo, hi)), aims[t][:, lo:hi], ALU.subtract
            )

        rounded = work.tile([P, RECALLED // P, H], BF16, name="rounded", tag="tab0", align_bytes=64)

        def round_x(turned, half, chunk):
            for b in range(BLOCKS):
                block = chunk * BLOCKS + b
                for inner in range(2):
                    first = b * HALF + inner * P
                    nc.tensor.transpose(
                        turned[:, first : first + P], x[2 * half + inner][:, block * P : (block + 1) * P], ident[:]
                    )
            rows = rounded[:, chunk * BLOCKS : (chunk + 1) * BLOCKS, :]
            nc.scalar.copy(
                rows.rearrange("j b (u g p e) -> j b u g p e", u=2, g=2, e=2)[:, :, :, half, :, :],
                turned[:].rearrange("j (b p u e) -> j b u p e", b=BLOCKS, u=2, e=2),
            )

        reduce_angles(0)
        for step in range(CHUNKS):
            make_terms(step)
            if step + 1 < CHUNKS:
                reduce_angles(step + 1)
            for inner in range(2):
                renew(step, inner)
        w2_mx.append(quantise_half("w2b", w2_raw[1], on_scalar))
        w3_mx.append(quantise_half("w3b", w3_raw[1], on_scalar))
        for t in range(2):
            reduce_angles(CHUNKS + t)
            recall(t, 0, RECALLED)
        for step in range(CHUNKS, len(STEPS)):
            for unit in range(CHUNKS + STEPS[step][1] // CHUNK, CHUNKS + STEPS[step][2] // CHUNK):
                make_terms(unit)
                if unit + 2 < 2 * CHUNKS:
                    reduce_angles(unit + 2)
            for inner in range(2):
                renew(step, inner)

        w4_codes, w4_sc = mx_tiles("w4", H)
        for half in range(2):
            cols = slice(half * HALF, (half + 1) * HALF)
            quantise_weight(w4_raw[half], w4_codes[:, cols], w4_sc[:, cols], nc.scalar.copy, staging())
        for chunk in range(RECALLED // CHUNK):
            round_x(banks[chunk % 2], 0, chunk)

        for lo, hi in ((0, CHUNK), (CHUNK, RECALLED)):
            for t in range(2, TILES):
                recall(t, lo, hi)

        x_codes = work.tile([P, RECALLED], U32, name="x_codes", tag="tab1", align_bytes=64)
        x_sc = keep.tile([P, RECALLED], U8, name="x_sc", align_bytes=64)

        def quantise_x(chunk, turned, words):
            round_x(turned, 1, chunk)
            for b in range(BLOCKS):
                pairs = rounded[:, chunk * BLOCKS + b, :].bitcast(F32)
                for u in range(2):
                    first = b * HALF + u * P
                    nc.tensor.transpose(words[:, first : first + P], pairs[:, u * P : (u + 1) * P], ident[:])
            grouped = staging()
            nc.scalar.copy(
                grouped.bitcast(F32).rearrange("p (b j u) -> p b j u", b=BLOCKS, u=2),
                words[:].rearrange("p (b u j) -> p b j u", b=BLOCKS, u=2),
            )
            cols = slice(chunk * CHUNK, (chunk + 1) * CHUNK)
            nc.vector.quantize_mx(x_codes[:, cols].bitcast(FP8X4), x_sc[:, cols], grouped)

        def mix(t, lo, hi, bank, y):
            channels = slice(t * P, (t + 1) * P)
            nc.tensor.matmul_mx(
                bank[:, : hi - lo], lhsT=w4_codes[:, channels].bitcast(FP8X4), lhsT_scale=w4_sc[:, channels],
                rhs=x_codes[:, lo:hi].bitcast(FP8X4), rhs_scale=x_sc[:, lo:hi], start=True, stop=True,
            )
            nc.vector.tensor_tensor(y, bank[:, : hi - lo], x[t][:, lo:hi], ALU.mult)

        def place(t, lo, hi, y):
            nc.vector.tensor_tensor(ration[t][:].indirect(entries(idx4, lo, hi)), y, wgo_sb[:, lo:hi], ALU.mult)
            if hi == RECALLED:
                nc.sync.dma_start(out[t * P : (t + 1) * P, :], ration[t][:])

        def features(part, mixed_banks):
            lo, hi = PARTS[part]
            ys = [bounded[part % 2 * TILES + t][:, : hi - lo] for t in range(TILES)]
            mix(0, lo, hi, banks[mixed_banks[0]], ys[0])
            for t in range(TILES):
                if t + 1 < TILES:
                    mix(t + 1, lo, hi, banks[mixed_banks[t + 1]], ys[t + 1])
                place(t, lo, hi, ys[t])

        quantise_x(0, banks[0], banks[1])
        features(0, (2, 3, 4, 5))
        for chunk, turned, words in ((1, 2, 6), (2, 3, 7), (3, 4, 1)):
            quantise_x(chunk, banks[turned], banks[words])
        features(1, (0, 5, 2, 3))
        features(2, (4, 6, 7, 1))
